import numpy as np, ml_dtypes
CORES = [24,25,26,27,28,29,30,31]
N = 8
BF = ml_dtypes.bfloat16
def gentries(a):
    return np.ascontiguousarray(a.reshape(8, 16, -1).transpose(0, 2, 1)).reshape(8, -1)
def gtable(e):
    e = np.asarray(e); return np.ascontiguousarray(e.reshape(8, -1, 16).transpose(0, 2, 1)).reshape(128, -1).astype(np.int32)
TT, P, R, S, CAP = 1024, 256, 2, 3, 24
def walk(planes, nbr, x, c):
    A = planes.astype(np.int64).reshape(N, 4, 4, TT).transpose(0, 3, 1, 2).reshape(N * TT, 4, 4); B = nbr.astype(np.int64).transpose(0, 2, 1).reshape(N * TT, 4)
    h = np.concatenate([x.astype(np.int64), np.ones((len(x), 1), np.int64)], 1); c = c.astype(np.int64); w = [c]
    for k in range(R):
        q = c // TT
        for s in range(S):
            v = np.einsum("mfc,mc->mf", A[c], h); face = np.argmin(v, 1)
            c = np.where((c // TT == q) & (np.min(v, 1) < 0), B[c, face], c)
        w.append(c)
    return np.stack(w)
def codes(rng, shape, own):
    r = np.arange(N).reshape(N, 1, 1); q = np.where(rng.random(shape) < own, r, (r + rng.integers(1, N, shape)) % N)
    return q * TT + rng.integers(0, TT, shape)
def mesh(rng, big, lo, hi):
    p = rng.integers(-big, big + 1, (N, 4, 4, TT)); p[:, :, 3] = rng.integers(lo, hi + 1, (N, 4, TT)); return p
def roomy(rng, p):
    h = np.stack([1 + rng.permutation(TT - 2)[:TT // 16] for r in range(N)]); k = h.shape[1]
    for r in range(N):
        u = p[r]; u[:, :3, h[r]] = rng.integers(-255, 256, (4, 3, k)); u[:, 3, h[r]] = rng.integers(3 * 255 * 1023, 2 ** 20 + 1, (4, k))
    return h
def choose(rng, p, h, b, x, c):
    big = int(np.abs(x).max()); r = np.arange(N).reshape(N, 1, 1)
    x = np.concatenate([x, rng.integers(-big, big + 1, (N, 8, P, 3))], 2); c = np.concatenate([c, r * TT + h[r, rng.integers(0, h.shape[1], (N, 8, P))]], 2)
    planes = p.reshape(N, 16, TT).astype(np.int32); m = c.shape[2]
    w = walk(planes, b, x.reshape(-1, 3), c.reshape(-1))[:R].reshape(R, N, 8, m) // TT
    cap = np.where(np.eye(N, dtype=bool), P, CAP); cnt = np.zeros((R, N, 8, N), np.int64); n = np.zeros((N, 8), np.int64); keep = np.zeros((N, 8, m), bool)
    k, i, g = np.ogrid[:R, :N, :8]
    for j in range(m):
        q = w[:, :, :, j]; ok = np.all(cnt[k, i, g, q] < cap[i, q], axis=0) & (n < P)
        cnt[k, i, g, q] += ok; n += ok; keep[:, :, j] = ok
    e = rng.permuted(np.nonzero(keep.reshape(N * 8, m))[1].reshape(N, 8, P), axis=2)
    x = np.take_along_axis(x, e[:, :, :, None], 2); c = np.take_along_axis(c, e, 2)
    return {"planes": planes, "nbr": b.astype(np.int32), "pts": np.ascontiguousarray(x.transpose(0, 1, 3, 2)).reshape(N, 24, P).astype(np.int32), "tet0": np.stack([gtable(u) for u in c])}
def setup_inputs(rng):
    p = mesh(rng, 127, -20000, 60000); h = roomy(rng, p)
    return choose(rng, p, h, codes(rng, (N, 4, TT), 0.6), rng.integers(-255, 256, (N, 8, 3 * P, 3)), codes(rng, (N, 8, 3 * P), 0.5))
def setup_inputs_full(rng):
    p = mesh(rng, 127, -20000, 60000); h = roomy(rng, p); r = np.arange(N).reshape(N, 1, 1); m = (N - 1) * CAP
    q = np.broadcast_to((r + 1 + np.arange(m) // CAP) % N, (N, 8, m)); c = q * TT + h[q, rng.integers(0, h.shape[1], (N, 8, m))]
    c = np.where(np.arange(8).reshape(1, 8, 1) % 2 == 0, c, codes(rng, (N, 8, m), 0.0)); c = np.concatenate([c, codes(rng, (N, 8, 2 * P), 0.8)], 2)
    return choose(rng, p, h, codes(rng, (N, 4, TT), 0.6), rng.integers(-255, 256, (N, 8, m + 2 * P, 3)), c)
def setup_inputs_ties(rng):
    p = mesh(rng, 1, -1, 2)
    p[:, 3] = np.where(rng.random((N, 1, TT)) < 0.5, p[:, 1], p[:, 3]); p[:, 2] = np.where(rng.random((N, 1, TT)) < 0.5, p[:, 0], p[:, 2]); h = roomy(rng, p)
    return choose(rng, p, h, codes(rng, (N, 4, TT), 0.6), rng.integers(-2, 3, (N, 8, 3 * P, 3)), codes(rng, (N, 8, 3 * P), 0.5))
def setup_inputs_few(rng):
    p = mesh(rng, 127, -20000, 60000); h = roomy(rng, p); b = codes(rng, (N, 4, TT), 1.0); q = rng.integers(0, N); b[q] = codes(rng, (N, 4, TT), 0.3)[q]
    c = codes(rng, (N, 8, 3 * P), 1.0); out = []
    for v in (b, c):
        u = rng.random(v.shape); out.append(np.where(u < 0.2, v // TT * TT, np.where(u < 0.4, v // TT * TT + TT - 1, v)))
    b, c = out; x = rng.integers(-255, 256, (N, 8, 3 * P, 3)); one = rng.random((N, 8, 3 * P)) < 0.4
    c = np.where(one, c[:, :, :1], c); x = np.where(one[:, :, :, None], x[:, :, :1], x)
    return choose(rng, p, h, b, x, c)
def setup_inputs_spread(rng):
    def some(bits, top, shape, plus):
        v = np.minimum(np.floor(np.exp2(bits * rng.random(shape))).astype(np.int64), top); v = np.where(rng.random(shape) < 0.125, top, v)
        return np.where(rng.random(shape) < plus, v, -v)
    p = some(10, 1023, (N, 4, 4, TT), 0.5); p[:, :, 3] = some(20, 2 ** 20, (N, 4, TT), 0.75); h = roomy(rng, p)
    return choose(rng, p, h, codes(rng, (N, 4, TT), 0.6), some(10, 1023, (N, 8, 3 * P, 3), 0.5), codes(rng, (N, 8, 3 * P), 0.5))
def points(pts, tet0):
    return pts.reshape(N, 8, 3, P).transpose(0, 1, 3, 2).reshape(-1, 3), np.stack([gentries(a) for a in tet0]).reshape(-1)
def check_inputs(d):
    bad = []; p = d["planes"].astype(np.int64).reshape(N, 4, 4, TT)
    if np.abs(p[:, :, :3]).max() > 1023 or np.abs(p[:, :, 3]).max() > 2 ** 20: bad.append("planes out of range")
    if np.abs(d["pts"].astype(np.int64)).max() > 1023: bad.append("pts out of range")
    for a in ("nbr", "tet0"):
        if d[a].min() < 0 or d[a].max() >= N * TT: bad.append(a + " out of range")
    if bad: return bad
    x, c = points(d["pts"], d["tet0"]); w = walk(d["planes"], d["nbr"], x, c)[:R].reshape(R, N, 8, P) // TT
    for q in range(N):
        n = np.count_nonzero(w == q, axis=3); n[:, q] = 0
        if n.max() > CAP: bad.append("more than CAP points of a group on rank " + str(q))
    return bad
def reference(planes, nbr, pts, tet0):
    x, c = points(pts, tet0); e = walk(planes, nbr, x, c)[R].reshape(N, 8, P)
    return {"y": np.stack([gtable(u) for u in e]).astype(np.float32)}

@@ -1,0 +1,452 @@
+from concourse.bass import DstId, RemoteDMATransfer
+from concourse.mybir import AluOpType, ActivationFunctionType
+
+OP = AluOpType
+ACT = ActivationFunctionType
+N, TT, P, R, S, CAP = 8, 1024, 256, 2, 3, 24
+NO = N - 1
+KF = NO * CAP
+KW = 192
+OFF = 32
+BIG = 16384.0
+BIGS = 4096.0
+PADL = 4
+TW = TT + 2 * PADL
+NR = CAP // 4
+EARLY = (1, 2)
+HALVES = {"o": ((0, 128, 0, 4), (128, 128, 8, 4)), "f": ((0, 96, 0, 3), (96, 80, 6, 3))}
+
+SCRATCH = {}
+
+
+def declare(where, shape, dtype, names):
+    for n in names.split():
+        SCRATCH[n] = (where, shape, dtype)
+
+
+declare("sbuf", [128, TW], "int32", "pl")
+declare("sbuf", [128, TW], "bfloat16", "nb")
+declare("dram", [256, 32], "bfloat16", "nbt")
+declare("sbuf", [128, 32], "int32", "nbi")
+declare("sbuf", [128, 64], "bfloat16", "nbs")
+declare("sbuf", [128, 32], "float32", "nbf fx w2")
+declare("sbuf", [128, P], "int32", "xi")
+declare("sbuf", [128, P], "bfloat16", "xt coord mask gm pay oy onb osb")
+declare("sbuf", [128, P], "float32", "ocrd opr")
+declare("sbuf", [128, KW], "bfloat16", "fy fnb fsb rq0 rq1")
+declare("sbuf", [128, KW], "float32", "fcrd fpr")
+declare("sbuf", [128, P + 48], "bfloat16", "win0 win1")
+declare("sbuf", [128, 42], "bfloat16", "pk0 pk1")
+declare("sbuf", [128, 16], "int32", "l0 fi ow si sj")
+declare("sbuf", [128, 16], "float32", "l32 ff nv j16 tau oh sl sm yl")
+declare("sbuf", [128, 4], "float32", "tal")
+declare("sbuf", [128, 16], "uint16", "bc slu of2 oidx fidx")
+declare("sbuf", [128, 32], "bfloat16", "lhl")
+declare("sbuf", [128, 512], "bfloat16", "ex mQ mL")
+declare("sbuf", [128, 1], "int32", "ki")
+declare("sbuf", [128, 112], "int32", "qc")
+declare("sbuf", [128, 112], "float32", "d0a d0 sc")
+declare("sbuf", [128, 112], "bfloat16", "oo")
+declare("sbuf", [128, 128], "bfloat16", "c1 cg1 cyg cxg cxn cy8 cgh c4 mA1 mA2 mF1 mF2 mF mI mJ mC mB mU1 mU2 mU3 mU mRH mRL")
+declare("sbuf", [128, 128], "float32", "mA w")
+declare("sbuf", [128, 64], "float32", "w1")
+declare("sbuf", [128, KF], "bfloat16", "s4")
+declare("sbuf", [128, P + KF], "bfloat16", "tab send")
+declare("sbuf", [128, 4, 32], "float32", "otr0 otr1")
+declare("sbuf", [128, 3, 32], "float32", "ftr0 ftr1")
+declare("psum", [128, 512], "float32", "pd0 pd1 pp0 pp1 pst px")
+declare("psum", [128, 16, 32], "float32", "pc0 pc1")
+SEMAPHORES = (["cv", "ct", "cs", "cg", "dl0", "dni", "dxi", "dpl", "dnt", "dnb", "dy"]
+              + [s + str(r) for s in ("rqs", "rss", "lq", "lr") for r in range(R)])
+
+
+def rank_program(g, core, T, topo):
+    rank = T.rank_of(core)
+    if rank is None:
+        return
+    base = rank * TT
+    others = [q for q in range(N) if q != rank]
+    queue = {"v": g.vector, "t": g.tensor, "s": g.scalar, "g": g, "y": g.sync}
+    own_sem = {"v": "cv", "t": "ct", "s": "cs", "g": "cg"}
+    count, waited, acc = {}, {}, {}
+
+    def wait(q, sem, val):
+        if waited.get((q, sem), 0) < val:
+            queue[q].wait_ge(T.sem[sem], val)
+            waited[(q, sem)] = val
+
+    def hazards(q, reads, writes):
+        need = {}
+        for kind, regs in (("r", reads), ("w", writes)):
+            for b, lo, hi in regs:
+                for l2, h2, k2, q2, sem, val in acc.get(b, []):
+                    if l2 < hi and lo < h2 and (kind == "w" or k2 == "w"):
+                        if q == "t" and q2 == "t" and k2 == "w" and kind == "w":
+                            continue
+                        need[sem] = max(need.get(sem, 0), val)
+        for sem in need:
+            wait(q, sem, need[sem])
+
+    def note(q, reads, writes, sem, val):
+        for kind, regs in (("r", reads), ("w", writes)):
+            for b, lo, hi in regs:
+                old = acc.get(b, [])
+                if kind == "w":
+                    old = [a for a in old if not (lo <= a[0] and a[1] <= hi)]
+                acc[b] = old + [(lo, hi, kind, q, sem, val)]
+
+    def do(q, fn, reads, writes):
+        hazards(q, reads, writes)
+        sem = own_sem[q]
+        count[sem] = count.get(sem, 0) + 1
+        fn(queue[q]).then_inc(T.sem[sem], 1)
+        note(q, reads, writes, sem, count[sem])
+
+    def full(*names):
+        return [(n, 0, 1 << 20) for n in names]
+
+    def dma(q, sem, out, in_, reads, writes, total):
+        hazards(q, reads, writes)
+        queue[q].dma_start(out, in_).then_inc(T.sem[sem], 16)
+        count[sem] = count.get(sem, 0) + 16
+        note("d", reads, writes, sem, total)
+
+    def ts(out, in0, s1, s2, ops, reads, writes):
+        if s2 is None:
+            do("v", lambda e: e.tensor_scalar(out, in0, s1, None, ops[0]), reads, writes)
+        else:
+            do("v", lambda e: e.tensor_scalar(out, in0, s1, s2, ops[0], ops[1]), reads, writes)
+
+    def tt(out, a, b, op, reads, writes):
+        do("v", lambda e: e.tensor_tensor(out, a, b, op), reads, writes)
+
+    def copy(out, in_, reads, writes):
+        do("v", lambda e: e.tensor_copy(out, in_), reads, writes)
+
+    def fill(ap, c, writes):
+        do("v", lambda e: e.memset(ap, c), [], writes)
+
+    def act(out, in_, func, reads, writes, **kw):
+        do("s", lambda e: e.activation(out, in_, func, **kw), reads, writes)
+
+    def mm(out, lhsT, rhs, start, stop, reads, writes):
+        do("t", lambda e: e.matmul(out, lhsT, rhs, start, stop), reads, writes)
+
+    fill(T.xi[:], 0, full("xi"))
+    fill(T.pl[:, 0:PADL], 0, [("pl", 0, PADL)])
+    fill(T.pl[:, TT + PADL:TW], 0, [("pl", TT + PADL, TW)])
+    dma("y", "dl0", T.l0[:], T.tet0[:], [], full("l0"), 16)
+    dma("s", "dni", T.nbi[:], T.nbr[:], [], full("nbi"), 16)
+    hazards("y", [], full("xi"))
+    hazards("s", [], full("xi"))
+    for c in range(3):
+        for h, q in ((9, "y"), (13, "s")):
+            dma(q, "dxi", T.xi[h + c:128:16, :], T.pts[c:24:3, :], [], full("xi%d" % (h + c)), 96)
+    XI = full("xi", *["xi%d" % h for h in (9, 10, 11, 13, 14, 15)])
+    for k in range(8):
+        dma("ys"[k % 2], "dpl", T.pl[16 * k:16 * k + 16, PADL:PADL + TT], T.planes[:], [], full("pl%d" % k), 128)
+    PL = full("pl", *["pl%d" % k for k in range(8)])
+
+    def iota(name, ap, pattern, b=0, ch=0, reg=None):
+        kw = {} if SCRATCH[name][2] == "int32" else {"allow_small_or_imprecise_dtypes": True}
+        do("g", lambda e: e.iota(ap, pattern, b, ch, **kw), [], reg or full(name))
+
+    def choose(name, src, pattern, cmp, fill_, b):
+        do("g", lambda e: e.affine_select(T[name][:], T[src][:], pattern, cmp, fill_, b, 0), full(src), full(name))
+
+    iota("ki", T.ki[:], [[0, 1]], 0, 1)
+    iota("c1", T.c1[:], [[1, 128]], 1)
+    iota("cg1", T.cg1[:], [[1, 8], [0, 16]], 1)
+    iota("nv", T.nv[:], [[1, 16]], 1)
+    iota("j16", T.j16[:], [[16, 16]], 0, 1)
+    if rank > 0:
+        iota("qc", T.qc[:, 0:16 * rank], [[1, rank], [0, 16]], 0, 0, [("qc", 0, 16 * rank)])
+    if rank < NO:
+        iota("qc", T.qc[:, 16 * rank:112], [[1, NO - rank], [0, 16]], rank + 1, 0, [("qc", 16 * rank, 112)])
+    iota("d0a", T.d0a[:], [[CAP, NO], [0, 16]], P - 1 - int(BIGS))
+    choose("d0", "d0a", [[0, NO], [1, 16]], OP.is_equal, -1000000.0, 0)
+    iota("cyg", T.cyg[:], [[4, 8], [0, 4], [1, 4]])
+    iota("cxg", T.cxg[:], [[4, 8], [1, 4], [0, 4]])
+    choose("cxn", "cxg", [[0, 8], [1, 4], [-1, 4]], OP.not_equal, -1.0, 0)
+    choose("cy8", "cyg", [[0, 8], [-1, 16]], OP.is_ge, -1.0, 7)
+    choose("cgh", "cg1", [[0, 8], [1, 16]], OP.is_ge, -1.0, -8)
+    iota("c4", T.c4[:], [[16, 8], [0, 4], [1, 4]], 1)
+    iota("s4", T.s4[:], [[0, KF // 4], [1, 4]])
+
+    fill(T.nb[:], 0.0, full("nb"))
+    sh, an = OP.logical_shift_right, OP.bitwise_and
+    ints = [(an, 112, None, 0), (an, 15, None, 0), (sh, 4, None, 0), (sh, 0, None, 0),
+            (sh, 2, None, 0), (an, 3, None, 0), (sh, 2, an, 1), (sh, 3, an, 1),
+            (sh, 4, an, 1), (an, 96, None, 0), (sh, 2, an, 3)]
+    for c, (o0, n0, o1, n1) in enumerate(ints):
+        ts(T.fi[:, c:c + 1], T.ki[:], n0, None if o1 is None else n1, (o0, o1), full("ki"), [("fi", c, c + 1)])
+    copy(T.ff[:, 0:11], T.fi[:, 0:11], [("fi", 0, 11)], full("ff"))
+    K16G, K15, KG, K0, KFC, M3, B2, B3, PAR, A32, XF = [T.ff[:, c:c + 1] for c in range(11)]
+
+    def fcol(c):
+        return T.fx[:, c:c + 1]
+
+    def dep(*cs):
+        return [("fx", c, c + 1) for c in cs]
+
+    def fx(c, in0, s1, s2, *ops):
+        ts(fcol(c), in0, s1, s2, ops, full("ff"), dep(c))
+
+    def tile(name, src, col, s2, ops, reads):
+        ts(T[name][:], T[src][:], col, s2, ops, full(src) + reads, full(name))
+
+    fx(0, K0, 1.0, None, OP.add)
+    fx(1, KG, 1.0, None, OP.add)
+    fx(2, K16G, -1.0, None, OP.mult)
+    EQ, EQM = (OP.is_equal,), (OP.is_equal, OP.mult)
+    tile("mB", "cg1", fcol(1), None, EQ, dep(1))
+    tile("mU1", "c1", fcol(0), -1.0, (OP.is_lt, OP.mult), dep(0))
+    tile("mU3", "c1", fcol(0), BIGS, EQM, dep(0))
+    tt(T.mU2[:], T.mU1[:], T.mB[:], OP.mult, full("mU1", "mB"), full("mU2"))
+    ts(T.bc[:, 0:8], T.nv[:, 0:8], 0.0, K15, (OP.mult, OP.add), full("nv", "ff"), full("bc"))
+    tt(T.mU[:], T.mU2[:], T.mU3[:], OP.add, full("mU2", "mU3"), full("mU"))
+    ts(T.oh[:], T.nv[:], -1.0, K15, (OP.add, OP.is_equal), full("nv", "ff"), full("oh"))
+    ts(T.w[:, 0:16], T.j16[:], fcol(2), None, (OP.add,), full("j16") + dep(2), [("w", 0, 16)])
+    fx(3, K16G, 9.0, None, OP.add)
+    fx(4, K16G, 13.0, None, OP.add)
+    fx(5, B2, -1.0, None, OP.mult)
+    tile("mI", "c1", fcol(0), None, EQ, dep(0))
+    tile("mRH", "c1", fcol(3), None, EQ, dep(3))
+    tile("mRL", "c1", fcol(4), None, EQ, dep(4))
+    fill(T.send[:, P:P + KF], 0.0, [("send", P, P + KF)])
+
+    def owners_to_slots(between):
+        tt(T.oo[:], T.ow[:].indirect(T.bc[:, 0:NO]), T.qc[:], OP.is_equal, full("ow", "bc", "qc"), full("oo"))
+        mm(T.pst[:, 0:112], T.mB[:], T.oo[:], True, True, full("mB", "oo"), full("pst"))
+        mm(T.pst[:, 128:240], T.mU[:], T.oo[:], True, True, full("mU", "oo"), full("pst"))
+        between()
+        do("v", lambda e: e.tensor_tensor_scan(T.sc[:], T.d0[:], T.pst[:, 0:112], -1000000.0, OP.max, OP.add), full("d0", "pst"), full("sc"))
+        tt(T.w[:, 16:128], T.pst[:, 128:240], T.sc[:], OP.add, full("pst", "sc"), [("w", 16, 128)])
+        tt(T.w1[:], T.w[:, 0:64], T.w[:, 64:128], OP.max, full("w"), full("w1"))
+        tt(T.w2[:], T.w1[:, 0:32], T.w1[:, 32:64], OP.max, full("w1"), full("w2"))
+        tt(T.sl[:], T.w2[:, 0:16], T.w2[:, 16:32], OP.max, full("w2"), full("sl"))
+        copy(T.slu[:], T.sl[:], full("sl"), full("slu"))
+
+    def remote(land, sem, lsem, src, at, width, to):
+        hazards("g", full(src), [])
+        tr = []
+        for d, q in enumerate(others):
+            dst = T.cores[q]
+            rid, pid, _ = topo.addr(dst)
+            e = topo.engines(core, dst)
+            me = rank - (rank > q)
+            tr.append(RemoteDMATransfer(dst_ids=[DstId(rid=rid, pnc=pid)], dma_engine_mask=(1 << e[2 * d]) | (1 << e[2 * d + 1]),
+                                        remote_sem=T.sem[sem], src=T[src][:, at + width * d:at + width * d + width],
+                                        dst=T[land][:, to + width * me:to + width * me + width]))
+        g.remote_dma_fused(tr, local_sem=T.sem[lsem])
+
+    def pack_and_send(r):
+        if r:
+            wait("v", "lq%d" % (r - 1), 2 * NO)
+        copy(T.send[:].indirect(T.slu[:]), T.pay[:], full("slu", "pay"), full("send"))
+        remote("rq%d" % r, "rqs%d" % r, "lq%d" % r, "send", P, CAP, 0)
+
+    def answer_places():
+        ts(T.si[:], T.sl[:], 3.0 * P, None, (OP.add,), full("sl"), full("si"))
+        ts(T.sj[:], T.si[:], 2, None, (OP.arith_shift_right,), full("si"), full("sj"))
+        tt(T.sm[:], T.sl[:], T.sj[:], OP.min, full("sl", "sj"), full("sm"))
+        copy(T.of2[:], T.sm[:], full("sm"), full("of2"))
+        act(T.mask[:], T.tab[:].indirect(T.slu[:]), ACT.Copy, full("tab", "slu"), full("mask"))
+
+    def rows_matmul(p, i, z, zname):
+        at, _, _, nb = HALVES[p][i]
+        n = 16 * nb
+        for h in range(2):
+            for e in range(2):
+                m = 128 * (2 * e + h)
+                mm(T["pc%d" % i][:, 0:nb, 16 * h:16 * h + 16], T.mL[:, m:m + 128], z[:, at + e * n:at + e * n + n],
+                   e == 0, e == 1, full("mL") + [(zname, at, at + 2 * n)], full("pc%d" % i))
+
+    def rows_transpose(p, i):
+        tr, nb = "%str%d" % (p, i), HALVES[p][i][3]
+        do("v", lambda e: e.transpose(T[tr][:], T["pc%d" % i][:, 0:nb, :]), full("pc%d" % i), full(tr))
+
+    def offsets(p, i):
+        _, _, lc, nb = HALVES[p][i]
+        tr = "%str%d" % (p, i)
+        for e in range(2):
+            c = lc + e * nb
+            ts(T[p + "idx"][:, c:c + nb], T[tr][:, :, e], float(PADL - OFF - base), float(TT + PADL), (OP.add, OP.min),
+               full(tr), [(p + "idx", c, c + nb)])
+
+    def walk(p, i, r, s0, s1):
+        at, k, lc, _ = HALVES[p][i]
+        end = at + k
+        pd, pp = "pd%d" % i, "pp%d" % i
+
+        def reg(name):
+            return [(name, at, end)]
+        for s in range(s0, s1):
+            z = ("pay" if p == "o" else "rq%d" % r) if s == 0 else p + "y"
+            y = "win%d" % r if p == "o" and s == S - 1 else p + "y"
+            idx = T[p + "idx"][:, lc:lc + k // 16]
+            idep = [(p + "idx", lc, lc + k // 16)]
+            tt(T[p + "pr"][:, at:end], T.pl[:].indirect(idx), T[p + "crd"][:, at:end], OP.mult, PL + idep + reg(p + "crd"), reg(p + "pr"))
+            act(T[p + "nb"][:, at:end], T.nb[:].indirect(idx), ACT.Copy, NB + idep, reg(p + "nb"))
+            mm(T[pp][:, 0:k], T.mJ[:], T[z][:, at:end], True, False, full("mJ") + reg(z), full(pp))
+            yield
+            mm(T[pd][:, 0:k], T.mA[:], T[p + "pr"][:, at:end], True, True, full("mA") + reg(p + "pr"), full(pd))
+            mm(T[pp][:, 0:k], T.mI[:], T[p + "nb"][:, at:end], False, False, full("mI") + reg(p + "nb"), full(pp))
+            yield
+            ts(T[p + "sb"][:, at:end], T[pd][:, 0:k], fcol(7), None, (OP.is_ge,), full(pd) + dep(7), reg(p + "sb"))
+            yield
+            mm(T[pp][:, 0:k], T.mF[:], T[p + "sb"][:, at:end], False, True, full("mF") + reg(p + "sb"), full(pp))
+            yield
+            ts(T[y][:, at:end], T[pp][:, 0:k], fcol(8), 0.0, (OP.add, OP.max), full(pp) + dep(8), reg(y))
+            yield
+            if s < S - 1:
+                rows_matmul(p, i, T[y], y)
+                yield
+                rows_transpose(p, i)
+                offsets(p, i)
+
+    def weave(*parts):
+        live = list(parts)
+        while live:
+            for w in list(live):
+                if next(w, 0) == 0:
+                    live.remove(w)
+
+    def own(r, s0, s1):
+        weave(*[walk("o", i, r, s0, s1) for i in range(2)])
+
+    def foreign_start(r, i):
+        rq = "rq%d" % r
+        at, k, _, _ = HALVES["f"][i]
+        pd = "pd%d" % i
+        rows_matmul("f", i, T[rq], rq)
+        mm(T[pd][:, 0:k], T.mC[:], T[rq][:, at:at + k], True, True, full("mC") + [(rq, at, at + k)], full(pd))
+        yield
+        rows_transpose("f", i)
+        act(T.fcrd[:, at:at + k], T[pd][:, 0:k], ACT.Identity, full(pd) + dep(9), [("fcrd", at, at + k)], bias=fcol(9))
+        offsets("f", i)
+        for _ in walk("f", i, r, 0, S):
+            yield
+
+    def foreign(r):
+        wait("t", "rqs%d" % r, 2 * NO)
+        weave(*[foreign_start(r, i) for i in range(2)])
+        pk = "pk%d" % r
+        for u in range(4):
+            mm(T.pst[:, 256:298], T.mQ[:, 128 * u:128 * u + 128], T.fy[:, u:KF:4], u == 0, u == 3, full("mQ", "fy"), full("pst"))
+        copy(T[pk][:], T.pst[:, 256:298], full("pst"), full(pk))
+        remote("win%d" % r, "rss%d" % r, "lr%d" % r, pk, 0, NR, P)
+
+    def merge(r):
+        win = "win%d" % r
+        wait("v", "rss%d" % r, 2 * NO)
+        for i in range(2):
+            at, k, lc, _ = HALVES["o"][i]
+            tt(T.gm[:, at:at + k], T[win][:, 0:P + 42].indirect(T.of2[:, lc:lc + 8]), T.mask[:, at:at + k], OP.mult,
+               full(win, "of2", "mask"), [("gm", at, at + k)])
+            rows_matmul("o", i, T.gm, "gm")
+        for i in range(2):
+            rows_transpose("o", i)
+
+    def from_lists(name, s1, s2, ops):
+        for i in range(2):
+            for e in range(2):
+                c = HALVES["o"][i][2] + 4 * e
+                tr = "otr%d" % i
+                ts(T[name][:, c:c + 4], T[tr][:, :, e], s1, s2, ops, full(tr), [(name, c, c + 4)])
+
+    copy(T.lhl[:, 0:16], T.l0[:], full("l0"), [("lhl", 0, 16)])
+    ts(T.l32[:], T.l0[:], float(OFF), None, (OP.add,), full("l0"), full("l32"))
+    ts(T.ow[:], T.l0[:], 10, None, (sh,), full("l0"), full("ow"))
+    tt(T.lhl[:, 16:32], T.l32[:], T.lhl[:, 0:16], OP.subtract, full("l32") + [("lhl", 0, 16)], [("lhl", 16, 32)])
+    for i in range(16):
+        act(T.ex[:, i:512:16], T.lhl[:], ACT.Identity, full("lhl", "oh"), full("ex%d" % i), scale=T.oh[:, i:i + 1])
+    EX = full(*["ex%d" % i for i in range(16)])
+
+    def coordinates():
+        ts(T.xt[:], T.xi[:], fcol(5), None, (OP.mult,), XI + dep(5), full("xt"))
+        tt(T.coord[:], T.xi[:], T.xt[:], OP.add, XI + full("xt"), full("coord"))
+
+    owners_to_slots(coordinates)
+    mm(T.px[:, 0:P], T.mI[:], T.coord[:], True, False, full("mI", "coord"), full("px"))
+    mm(T.px[:, 0:P], T.mRH[:], T.ex[:, 0:P], False, False, full("mRH") + EX, full("px"))
+    mm(T.px[:, 0:P], T.mRL[:], T.ex[:, P:2 * P], False, True, full("mRL") + EX, full("px"))
+    act(T.pay[:], T.px[:, 0:P], ACT.Identity, full("px"), full("pay"))
+    pack_and_send(0)
+
+    copy(T.nbs[:, 0:32], T.nbi[:], full("nbi"), [("nbs", 0, 32)])
+    ts(T.nbf[:], T.nbi[:], float(OFF), None, (OP.add,), full("nbi"), full("nbf"))
+    tt(T.nbs[:, 32:64], T.nbf[:], T.nbs[:, 0:32], OP.subtract, full("nbf") + [("nbs", 0, 32)], [("nbs", 32, 64)])
+    for h in range(2):
+        dma("y", "dnt", T.nbt[128 * h:128 * h + 128, :], T.nbs[:, 32 * h:32 * h + 32], full("nbs"), full("nbt%d" % h), 32)
+    hazards("y", full("nb"), [])
+    for k in range(8):
+        dma("y", "dnb", T.nb[16 * k:16 * k + 8, PADL:PADL + TT], T.nbt[:], full("nbt0", "nbt1"), full("nb%d" % k), 128)
+    NB = full("nb", *["nb%d" % k for k in range(8)])
+
+    ts(T.oidx[:], T.l0[:], float(PADL - base), float(TT + PADL), (OP.add, OP.min), full("l0"), full("oidx"))
+    fx(13, B2, 4.0, K16G, OP.mult, OP.add)
+    fx(14, B3, -1.0, 1.0, OP.mult, OP.add)
+    ts(fcol(10), M3, 0.0, fcol(14), (OP.is_equal, OP.max), full("ff") + dep(14), dep(10))
+    tt(fcol(7), XF, M3, OP.is_gt, full("ff"), dep(7))
+    tt(fcol(15), XF, M3, OP.is_equal, full("ff"), dep(15))
+    fx(8, B3, -BIG, -3.0 * BIG, OP.mult, OP.add)
+    fx(9, M3, 3.0, None, OP.is_equal)
+    ts(fcol(16), K16G, M3, B3, (OP.add, OP.mult), full("ff"), dep(16))
+    fx(18, PAR, -1.0, 1.0, OP.mult, OP.add)
+    ts(fcol(17), fcol(15), -2.0 * BIG, BIG, (OP.mult, OP.add), dep(15), dep(17))
+    ts(fcol(19), KG, 1.0, fcol(15), (OP.add, OP.mult), full("ff") + dep(15), dep(19))
+    tt(fcol(11), fcol(10), fcol(18), OP.mult, dep(10, 18), dep(11))
+    tt(fcol(12), fcol(10), PAR, OP.mult, full("ff") + dep(10), dep(12))
+    tile("mC", "c4", fcol(16), None, EQ, dep(16))
+    ts(T.tau[:, 0:9], T.nv[:, 0:9], fcol(13), fcol(10), (OP.add, OP.mult), full("nv") + dep(10, 13), full("tau"))
+    tile("mA1", "cyg", KFC, None, EQ, full("ff"))
+    tile("mA2", "cxn", KFC, None, EQ, full("ff"))
+    tile("mF1", "cy8", KFC, fcol(17), EQM, full("ff") + dep(17))
+    tile("mF2", "cgh", fcol(19), BIG, EQM, dep(19))
+    for h in range(2):
+        ts(T.tal[:, 2 * h:2 * h + 2], T.nv[:, 0:2], A32, fcol(11 + h), (OP.add, OP.mult), full("nv", "ff") + dep(11 + h), [("tal", 2 * h, 2 * h + 2)])
+    tt(T.mA[:], T.mA1[:], T.mA2[:], OP.subtract, full("mA1", "mA2"), full("mA"))
+    tt(T.mF[:], T.mF1[:], T.mF2[:], OP.add, full("mF1", "mF2"), full("mF"))
+    tile("mJ", "c1", T.tau[:, 8:9], None, EQ, full("tau"))
+    for e in range(2):
+        for h in range(2):
+            at = 128 * (2 * e + h)
+            ts(T.mL[:, at:at + 128], T.c1[:], T.tal[:, 2 * h + e:2 * h + e + 1], None, EQ, full("c1", "tal"), [("mL", at, at + 128)])
+    mm(T.px[:, 0:P], T.mC[:], T.coord[:], True, True, full("mC", "coord"), full("px"))
+    act(T.ocrd[:], T.px[:, 0:P], ACT.Identity, full("px") + dep(9), full("ocrd"), bias=fcol(9))
+    for r in range(R):
+        fill(T["rq%d" % r][:, KF:KW], 0.0, full("rq%d" % r))
+    fill(T.fy[:, KF:KW], 0.0, [("fy", KF, KW)])
+    for u in range(4):
+        ts(T.mQ[:, 128 * u:128 * u + 128], T.c1[:], T.tau[:, u:u + 1], None, EQ, full("c1", "tau"), [("mQ", 128 * u, 128 * u + 128)])
+    for h in range(2):
+        ts(T.tab[:, 128 * h:128 * h + 128], T.c1[:], 0.0, fcol(10), (OP.is_ge, OP.mult), full("c1") + dep(10), [("tab", 128 * h, 128 * h + 128)])
+    ts(T.tab[:, P:P + KF], T.s4[:], M3, fcol(14), EQM, full("s4", "ff") + dep(14), [("tab", P, P + KF)])
+    answer_places()
+
+    for r in range(R):
+        own(r, 0, EARLY[r])
+        foreign(r)
+        own(r, EARLY[r], S)
+        merge(r)
+        if r + 1 < R:
+            from_lists("ow", 1.0 / TT, -(OFF + 511.5) / TT, (OP.mult, OP.add))
+            mm(T.px[:, 0:P], T.mI[:], T.coord[:], True, False, full("mI", "coord"), full("px"))
+            mm(T.px[:, 0:P], T.mI[:], T.gm[:], False, True, full("mI", "gm"), full("px"))
+            act(T.pay[:], T.px[:, 0:P], ACT.Identity, full("px"), full("pay"))
+            owners_to_slots(lambda: None)
+            pack_and_send(r + 1)
+            offsets("o", 0)
+            offsets("o", 1)
+            answer_places()
+        else:
+            from_lists("yl", -float(OFF), None, (OP.add,))
+            dma("y", "dy", T.y[:], T.yl[:], full("yl"), [], 16)
+    for sem in ("ct", "cs", "cg"):
+        wait("g", sem, count[sem])
+    for sem in ("cv", "dl0", "dni", "dxi", "dpl", "dnt", "dnb", "dy"):
+        wait("y", sem, count[sem])
+    for r in range(R):
+        wait("g", "lq%d" % r, 2 * NO)
+        wait("g", "lr%d" % r, 2 * NO)

@@ -6,15 +6,16 @@ ACT = ActivationFunctionType
 N, TT, P, R, S, CAP = 8, 1024, 256, 2, 3, 24
 NO = N - 1
 KF = NO * CAP
-KW = 192
+KW = 176
 OFF = 32
 BIG = 16384.0
 BIGS = 4096.0
 PADL = 4
 TW = TT + 2 * PADL
 NR = CAP // 4
-EARLY = (1, 2)
-HALVES = {"o": ((0, 128, 0, 4), (128, 128, 8, 4)), "f": ((0, 96, 0, 3), (96, 80, 6, 3))}
+EARLY = (1, 1)
+HALVES = {"o": ((0, 128, 128, 0, 4), (128, 128, 128, 8, 4)), "f": ((0, 96, 96, 0, 6), (96, 80, 72, 6, 5))}
+SUB = {"o": 2, "f": 1}
 
 SCRATCH = {}
 
@@ -43,7 +44,8 @@ declare("sbuf", [128, 4], "float32", "tal")
 declare("sbuf", [128, 16], "uint16", "bc slu of2 oidx fidx")
 declare("sbuf", [128, 32], "bfloat16", "lhl")
 declare("sbuf", [128, 512], "bfloat16", "ex mQ mL")
-declare("sbuf", [128, 1], "int32", "ki")
+declare("sbuf", [128, 2], "int32", "ki")
+declare("sbuf", [128, 1], "float32", "k1")
 declare("sbuf", [128, 112], "int32", "qc")
 declare("sbuf", [128, 112], "float32", "d0a d0 sc")
 declare("sbuf", [128, 112], "bfloat16", "oo")
@@ -53,7 +55,8 @@ declare("sbuf", [128, 64], "float32", "w1")
 declare("sbuf", [128, KF], "bfloat16", "s4")
 declare("sbuf", [128, P + KF], "bfloat16", "tab send")
 declare("sbuf", [128, 4, 32], "float32", "otr0 otr1")
-declare("sbuf", [128, 3, 32], "float32", "ftr0 ftr1")
+declare("sbuf", [128, 6, 32], "float32", "ftr0")
+declare("sbuf", [128, 5, 32], "float32", "ftr1")
 declare("psum", [128, 512], "float32", "pd0 pd1 pp0 pp1 pst px")
 declare("psum", [128, 16, 32], "float32", "pc0 pc1")
 SEMAPHORES = (["cv", "ct", "cs", "cg", "dl0", "dni", "dxi", "dpl", "dnt", "dnb", "dy"]
@@ -133,8 +136,6 @@ def rank_program(g, core, T, topo):
         do("t", lambda e: e.matmul(out, lhsT, rhs, start, stop), reads, writes)
 
     fill(T.xi[:], 0, full("xi"))
-    fill(T.pl[:, 0:PADL], 0, [("pl", 0, PADL)])
-    fill(T.pl[:, TT + PADL:TW], 0, [("pl", TT + PADL, TW)])
     dma("y", "dl0", T.l0[:], T.tet0[:], [], full("l0"), 16)
     dma("s", "dni", T.nbi[:], T.nbr[:], [], full("nbi"), 16)
     hazards("y", [], full("xi"))
@@ -154,7 +155,8 @@ def rank_program(g, core, T, topo):
     def choose(name, src, pattern, cmp, fill_, b):
         do("g", lambda e: e.affine_select(T[name][:], T[src][:], pattern, cmp, fill_, b, 0), full(src), full(name))
 
-    iota("ki", T.ki[:], [[0, 1]], 0, 1)
+    iota("ki", T.ki[:], [[16, 2]], 0, 1)
+    iota("k1", T.k1[:], [[0, 1]], 1, 1)
     iota("c1", T.c1[:], [[1, 128]], 1)
     iota("cg1", T.cg1[:], [[1, 8], [0, 16]], 1)
     iota("nv", T.nv[:], [[1, 16]], 1)
@@ -173,15 +175,15 @@ def rank_program(g, core, T, topo):
     iota("c4", T.c4[:], [[16, 8], [0, 4], [1, 4]], 1)
     iota("s4", T.s4[:], [[0, KF // 4], [1, 4]])
 
-    fill(T.nb[:], 0.0, full("nb"))
     sh, an = OP.logical_shift_right, OP.bitwise_and
-    ints = [(an, 112, None, 0), (an, 15, None, 0), (sh, 4, None, 0), (sh, 0, None, 0),
-            (sh, 2, None, 0), (an, 3, None, 0), (sh, 2, an, 1), (sh, 3, an, 1),
-            (sh, 4, an, 1), (an, 96, None, 0), (sh, 2, an, 3)]
-    for c, (o0, n0, o1, n1) in enumerate(ints):
-        ts(T.fi[:, c:c + 1], T.ki[:], n0, None if o1 is None else n1, (o0, o1), full("ki"), [("fi", c, c + 1)])
-    copy(T.ff[:, 0:11], T.fi[:, 0:11], [("fi", 0, 11)], full("ff"))
-    K16G, K15, KG, K0, KFC, M3, B2, B3, PAR, A32, XF = [T.ff[:, c:c + 1] for c in range(11)]
+    K16G, K15, KG1, B2, KFC, M3, B3, PAR, A32, XF = [T.ff[:, c:c + 1] for c in range(10)]
+    EARLY_FF, LATE_FF = [("ff", 0, 4)], [("ff", 4, 10)]
+
+    def columns(ints, at):
+        for c, (src, o0, n0, o1, n1) in enumerate(ints):
+            ts(T.fi[:, at + c:at + c + 1], T.ki[:, src:src + 1], n0, None if o1 is None else n1, (o0, o1), full("ki"), [("fi", at + c, at + c + 1)])
+        end = at + len(ints)
+        copy(T.ff[:, at:end], T.fi[:, at:end], [("fi", at, end)], [("ff", at, end)])
 
     def fcol(c):
         return T.fx[:, c:c + 1]
@@ -190,39 +192,38 @@ def rank_program(g, core, T, topo):
         return [("fx", c, c + 1) for c in cs]
 
     def fx(c, in0, s1, s2, *ops):
-        ts(fcol(c), in0, s1, s2, ops, full("ff"), dep(c))
+        ts(fcol(c), in0, s1, s2, ops, EARLY_FF + LATE_FF, dep(c))
 
     def tile(name, src, col, s2, ops, reads):
         ts(T[name][:], T[src][:], col, s2, ops, full(src) + reads, full(name))
 
-    fx(0, K0, 1.0, None, OP.add)
-    fx(1, KG, 1.0, None, OP.add)
-    fx(2, K16G, -1.0, None, OP.mult)
     EQ, EQM = (OP.is_equal,), (OP.is_equal, OP.mult)
-    tile("mB", "cg1", fcol(1), None, EQ, dep(1))
-    tile("mU1", "c1", fcol(0), -1.0, (OP.is_lt, OP.mult), dep(0))
-    tile("mU3", "c1", fcol(0), BIGS, EQM, dep(0))
+    columns([(0, an, 112, None, 0), (0, an, 15, None, 0), (1, sh, 4, None, 0), (0, sh, 2, an, 1)], 0)
+    tile("mB", "cg1", KG1, None, EQ, EARLY_FF)
+    tile("mU1", "c1", T.k1[:], -1.0, (OP.is_lt, OP.mult), full("k1"))
+    tile("mU3", "c1", T.k1[:], BIGS, EQM, full("k1"))
     tt(T.mU2[:], T.mU1[:], T.mB[:], OP.mult, full("mU1", "mB"), full("mU2"))
-    ts(T.bc[:, 0:8], T.nv[:, 0:8], 0.0, K15, (OP.mult, OP.add), full("nv", "ff"), full("bc"))
+    ts(T.bc[:, 0:8], T.nv[:, 0:8], 0.0, K15, (OP.mult, OP.add), full("nv") + EARLY_FF, full("bc"))
     tt(T.mU[:], T.mU2[:], T.mU3[:], OP.add, full("mU2", "mU3"), full("mU"))
-    ts(T.oh[:], T.nv[:], -1.0, K15, (OP.add, OP.is_equal), full("nv", "ff"), full("oh"))
-    ts(T.w[:, 0:16], T.j16[:], fcol(2), None, (OP.add,), full("j16") + dep(2), [("w", 0, 16)])
-    fx(3, K16G, 9.0, None, OP.add)
-    fx(4, K16G, 13.0, None, OP.add)
-    fx(5, B2, -1.0, None, OP.mult)
-    tile("mI", "c1", fcol(0), None, EQ, dep(0))
-    tile("mRH", "c1", fcol(3), None, EQ, dep(3))
-    tile("mRL", "c1", fcol(4), None, EQ, dep(4))
+    ts(T.oh[:], T.nv[:], -1.0, K15, (OP.add, OP.is_equal), full("nv") + EARLY_FF, full("oh"))
+    ts(T.w[:, 0:16], T.j16[:], K16G, None, (OP.subtract,), full("j16") + EARLY_FF, [("w", 0, 16)])
+    tile("mI", "c1", T.k1[:], None, EQ, full("k1"))
+    tile("mRH", "c1", K16G, 9.0, (OP.subtract, OP.is_equal), EARLY_FF)
+    tile("mRL", "c1", K16G, 13.0, (OP.subtract, OP.is_equal), EARLY_FF)
     fill(T.send[:, P:P + KF], 0.0, [("send", P, P + KF)])
 
-    def owners_to_slots(between):
+    def owners_to_slots(*between):
+        todo = list(between) + [lambda: None] * 4
         tt(T.oo[:], T.ow[:].indirect(T.bc[:, 0:NO]), T.qc[:], OP.is_equal, full("ow", "bc", "qc"), full("oo"))
         mm(T.pst[:, 0:112], T.mB[:], T.oo[:], True, True, full("mB", "oo"), full("pst"))
-        mm(T.pst[:, 128:240], T.mU[:], T.oo[:], True, True, full("mU", "oo"), full("pst"))
-        between()
+        mm(T.pd0[:, 0:112], T.mU[:], T.oo[:], True, True, full("mU", "oo"), full("pd0"))
+        todo[0]()
         do("v", lambda e: e.tensor_tensor_scan(T.sc[:], T.d0[:], T.pst[:, 0:112], -1000000.0, OP.max, OP.add), full("d0", "pst"), full("sc"))
-        tt(T.w[:, 16:128], T.pst[:, 128:240], T.sc[:], OP.add, full("pst", "sc"), [("w", 16, 128)])
+        todo[1]()
+        tt(T.w[:, 16:128], T.pd0[:, 0:112], T.sc[:], OP.add, full("pd0", "sc"), [("w", 16, 128)])
+        todo[2]()
         tt(T.w1[:], T.w[:, 0:64], T.w[:, 64:128], OP.max, full("w"), full("w1"))
+        todo[3]()
         tt(T.w2[:], T.w1[:, 0:32], T.w1[:, 32:64], OP.max, full("w1"), full("w2"))
         tt(T.sl[:], T.w2[:, 0:16], T.w2[:, 16:32], OP.max, full("w2"), full("sl"))
         copy(T.slu[:], T.sl[:], full("sl"), full("slu"))
@@ -254,56 +255,58 @@ def rank_program(g, core, T, topo):
         act(T.mask[:], T.tab[:].indirect(T.slu[:]), ACT.Copy, full("tab", "slu"), full("mask"))
 
     def rows_matmul(p, i, z, zname):
-        at, _, _, nb = HALVES[p][i]
+        at, _, _, _, nb = HALVES[p][i]
         n = 16 * nb
         for h in range(2):
-            for e in range(2):
+            for e in range(SUB[p]):
                 m = 128 * (2 * e + h)
                 mm(T["pc%d" % i][:, 0:nb, 16 * h:16 * h + 16], T.mL[:, m:m + 128], z[:, at + e * n:at + e * n + n],
-                   e == 0, e == 1, full("mL") + [(zname, at, at + 2 * n)], full("pc%d" % i))
+                   e == 0, e == SUB[p] - 1, full("mL") + [(zname, at, at + SUB[p] * n)], full("pc%d" % i))
 
     def rows_transpose(p, i):
-        tr, nb = "%str%d" % (p, i), HALVES[p][i][3]
+        tr, nb = "%str%d" % (p, i), HALVES[p][i][4]
         do("v", lambda e: e.transpose(T[tr][:], T["pc%d" % i][:, 0:nb, :]), full("pc%d" % i), full(tr))
 
     def offsets(p, i):
-        _, _, lc, nb = HALVES[p][i]
+        lc, nb = HALVES[p][i][3:5]
         tr = "%str%d" % (p, i)
-        for e in range(2):
+        for e in range(SUB[p]):
             c = lc + e * nb
             ts(T[p + "idx"][:, c:c + nb], T[tr][:, :, e], float(PADL - OFF - base), float(TT + PADL), (OP.add, OP.min),
                full(tr), [(p + "idx", c, c + nb)])
 
     def walk(p, i, r, s0, s1):
-        at, k, lc, _ = HALVES[p][i]
-        end = at + k
+        at, kg, k, lc, _ = HALVES[p][i]
         pd, pp = "pd%d" % i, "pp%d" % i
+        end, gend = at + k, at + kg
 
         def reg(name):
-            return [(name, at, end)]
+            return [(name, at, gend)]
         for s in range(s0, s1):
             z = ("pay" if p == "o" else "rq%d" % r) if s == 0 else p + "y"
             y = "win%d" % r if p == "o" and s == S - 1 else p + "y"
-            idx = T[p + "idx"][:, lc:lc + k // 16]
-            idep = [(p + "idx", lc, lc + k // 16)]
-            tt(T[p + "pr"][:, at:end], T.pl[:].indirect(idx), T[p + "crd"][:, at:end], OP.mult, PL + idep + reg(p + "crd"), reg(p + "pr"))
-            act(T[p + "nb"][:, at:end], T.nb[:].indirect(idx), ACT.Copy, NB + idep, reg(p + "nb"))
+            idx = T[p + "idx"][:, lc:lc + kg // 16]
+            idep = [(p + "idx", lc, lc + kg // 16)]
+            tt(T[p + "pr"][:, at:gend], T.pl[:].indirect(idx), T[p + "crd"][:, at:gend], OP.mult, PL + idep + reg(p + "crd"), reg(p + "pr"))
+            act(T[p + "nb"][:, at:gend], T.nb[:].indirect(idx), ACT.Copy, NB + idep, reg(p + "nb"))
             mm(T[pp][:, 0:k], T.mJ[:], T[z][:, at:end], True, False, full("mJ") + reg(z), full(pp))
             yield
             mm(T[pd][:, 0:k], T.mA[:], T[p + "pr"][:, at:end], True, True, full("mA") + reg(p + "pr"), full(pd))
-            mm(T[pp][:, 0:k], T.mI[:], T[p + "nb"][:, at:end], False, False, full("mI") + reg(p + "nb"), full(pp))
             yield
             ts(T[p + "sb"][:, at:end], T[pd][:, 0:k], fcol(7), None, (OP.is_ge,), full(pd) + dep(7), reg(p + "sb"))
             yield
+            mm(T[pp][:, 0:k], T.mI[:], T[p + "nb"][:, at:end], False, False, full("mI") + reg(p + "nb"), full(pp))
             mm(T[pp][:, 0:k], T.mF[:], T[p + "sb"][:, at:end], False, True, full("mF") + reg(p + "sb"), full(pp))
             yield
-            ts(T[y][:, at:end], T[pp][:, 0:k], fcol(8), 0.0, (OP.add, OP.max), full(pp) + dep(8), reg(y))
+            ts(T[y][:, at:end], T[pp][:, 0:k], fcol(8), 0.0, (OP.add, OP.max), full(pp) + dep(8), [(y, at, end)])
             yield
             if s < S - 1:
                 rows_matmul(p, i, T[y], y)
                 yield
                 rows_transpose(p, i)
+                yield
                 offsets(p, i)
+                yield
 
     def weave(*parts):
         live = list(parts)
@@ -317,14 +320,16 @@ def rank_program(g, core, T, topo):
 
     def foreign_start(r, i):
         rq = "rq%d" % r
-        at, k, _, _ = HALVES["f"][i]
-        pd = "pd%d" % i
+        at, kg, k, _, _ = HALVES["f"][i]
+        pp = "pp%d" % i
         rows_matmul("f", i, T[rq], rq)
-        mm(T[pd][:, 0:k], T.mC[:], T[rq][:, at:at + k], True, True, full("mC") + [(rq, at, at + k)], full(pd))
         yield
+        mm(T[pp][:, 0:kg], T.mC[:], T[rq][:, at:at + kg], True, True, full("mC") + [(rq, at, at + kg)], full(pp))
         rows_transpose("f", i)
-        act(T.fcrd[:, at:at + k], T[pd][:, 0:k], ACT.Identity, full(pd) + dep(9), [("fcrd", at, at + k)], bias=fcol(9))
+        act(T.fcrd[:, at:at + kg], T[pp][:, 0:kg], ACT.Identity, full(pp) + dep(9), [("fcrd", at, at + kg)], bias=fcol(9))
+        yield
         offsets("f", i)
+        yield
         for _ in walk("f", i, r, 0, S):
             yield
 
@@ -341,7 +346,7 @@ def rank_program(g, core, T, topo):
         win = "win%d" % r
         wait("v", "rss%d" % r, 2 * NO)
         for i in range(2):
-            at, k, lc, _ = HALVES["o"][i]
+            at, k, _, lc, _ = HALVES["o"][i]
             tt(T.gm[:, at:at + k], T[win][:, 0:P + 42].indirect(T.of2[:, lc:lc + 8]), T.mask[:, at:at + k], OP.mult,
                full(win, "of2", "mask"), [("gm", at, at + k)])
             rows_matmul("o", i, T.gm, "gm")
@@ -351,7 +356,7 @@ def rank_program(g, core, T, topo):
     def from_lists(name, s1, s2, ops):
         for i in range(2):
             for e in range(2):
-                c = HALVES["o"][i][2] + 4 * e
+                c = HALVES["o"][i][3] + 4 * e
                 tr = "otr%d" % i
                 ts(T[name][:, c:c + 4], T[tr][:, :, e], s1, s2, ops, full(tr), [(name, c, c + 4)])
 
@@ -364,57 +369,67 @@ def rank_program(g, core, T, topo):
     EX = full(*["ex%d" % i for i in range(16)])
 
     def coordinates():
-        ts(T.xt[:], T.xi[:], fcol(5), None, (OP.mult,), XI + dep(5), full("xt"))
-        tt(T.coord[:], T.xi[:], T.xt[:], OP.add, XI + full("xt"), full("coord"))
+        ts(T.xt[:], T.xi[:], B2, None, (OP.mult,), XI + EARLY_FF, full("xt"))
+        tt(T.coord[:], T.xi[:], T.xt[:], OP.subtract, XI + full("xt"), full("coord"))
 
-    owners_to_slots(coordinates)
+    def codes0():
+        copy(T.nbs[:, 0:32], T.nbi[:], full("nbi"), [("nbs", 0, 32)])
+
+    def codes1():
+        ts(T.nbf[:], T.nbi[:], float(OFF), None, (OP.add,), full("nbi"), full("nbf"))
+
+    def codes2():
+        tt(T.nbs[:, 32:64], T.nbf[:], T.nbs[:, 0:32], OP.subtract, full("nbf") + [("nbs", 0, 32)], [("nbs", 32, 64)])
+        for h in range(2):
+            dma("y", "dnt", T.nbt[128 * h:128 * h + 128, :], T.nbs[:, 32 * h:32 * h + 32], full("nbs"), full("nbt%d" % h), 32)
+
+    owners_to_slots(coordinates, codes0, codes1, codes2)
     mm(T.px[:, 0:P], T.mI[:], T.coord[:], True, False, full("mI", "coord"), full("px"))
     mm(T.px[:, 0:P], T.mRH[:], T.ex[:, 0:P], False, False, full("mRH") + EX, full("px"))
     mm(T.px[:, 0:P], T.mRL[:], T.ex[:, P:2 * P], False, True, full("mRL") + EX, full("px"))
     act(T.pay[:], T.px[:, 0:P], ACT.Identity, full("px"), full("pay"))
     pack_and_send(0)
 
-    copy(T.nbs[:, 0:32], T.nbi[:], full("nbi"), [("nbs", 0, 32)])
-    ts(T.nbf[:], T.nbi[:], float(OFF), None, (OP.add,), full("nbi"), full("nbf"))
-    tt(T.nbs[:, 32:64], T.nbf[:], T.nbs[:, 0:32], OP.subtract, full("nbf") + [("nbs", 0, 32)], [("nbs", 32, 64)])
-    for h in range(2):
-        dma("y", "dnt", T.nbt[128 * h:128 * h + 128, :], T.nbs[:, 32 * h:32 * h + 32], full("nbs"), full("nbt%d" % h), 32)
+    fill(T.nb[:], 0.0, full("nb"))
     hazards("y", full("nb"), [])
     for k in range(8):
         dma("y", "dnb", T.nb[16 * k:16 * k + 8, PADL:PADL + TT], T.nbt[:], full("nbt0", "nbt1"), full("nb%d" % k), 128)
     NB = full("nb", *["nb%d" % k for k in range(8)])
-
+    fill(T.pl[:, 0:PADL], 0, [("pl", 0, PADL)])
+    fill(T.pl[:, TT + PADL:TW], 0, [("pl", TT + PADL, TW)])
+    columns([(0, sh, 2, None, 0), (0, an, 3, None, 0), (0, sh, 3, an, 1), (0, sh, 4, an, 1), (0, an, 96, None, 0),
+             (0, sh, 2, an, 3)], 4)
     ts(T.oidx[:], T.l0[:], float(PADL - base), float(TT + PADL), (OP.add, OP.min), full("l0"), full("oidx"))
     fx(13, B2, 4.0, K16G, OP.mult, OP.add)
     fx(14, B3, -1.0, 1.0, OP.mult, OP.add)
-    ts(fcol(10), M3, 0.0, fcol(14), (OP.is_equal, OP.max), full("ff") + dep(14), dep(10))
-    tt(fcol(7), XF, M3, OP.is_gt, full("ff"), dep(7))
-    tt(fcol(15), XF, M3, OP.is_equal, full("ff"), dep(15))
+    ts(fcol(10), M3, 0.0, fcol(14), (OP.is_equal, OP.max), LATE_FF + dep(14), dep(10))
+    tt(fcol(7), XF, M3, OP.is_gt, LATE_FF, dep(7))
+    tt(fcol(15), XF, M3, OP.is_equal, LATE_FF, dep(15))
     fx(8, B3, -BIG, -3.0 * BIG, OP.mult, OP.add)
     fx(9, M3, 3.0, None, OP.is_equal)
-    ts(fcol(16), K16G, M3, B3, (OP.add, OP.mult), full("ff"), dep(16))
+    ts(fcol(16), K16G, M3, B3, (OP.add, OP.mult), EARLY_FF + LATE_FF, dep(16))
     fx(18, PAR, -1.0, 1.0, OP.mult, OP.add)
     ts(fcol(17), fcol(15), -2.0 * BIG, BIG, (OP.mult, OP.add), dep(15), dep(17))
-    ts(fcol(19), KG, 1.0, fcol(15), (OP.add, OP.mult), full("ff") + dep(15), dep(19))
+    tt(fcol(19), KG1, fcol(15), OP.mult, EARLY_FF + dep(15), dep(19))
     tt(fcol(11), fcol(10), fcol(18), OP.mult, dep(10, 18), dep(11))
-    tt(fcol(12), fcol(10), PAR, OP.mult, full("ff") + dep(10), dep(12))
+    tt(fcol(12), fcol(10), PAR, OP.mult, LATE_FF + dep(10), dep(12))
     tile("mC", "c4", fcol(16), None, EQ, dep(16))
     ts(T.tau[:, 0:9], T.nv[:, 0:9], fcol(13), fcol(10), (OP.add, OP.mult), full("nv") + dep(10, 13), full("tau"))
-    tile("mA1", "cyg", KFC, None, EQ, full("ff"))
-    tile("mA2", "cxn", KFC, None, EQ, full("ff"))
-    tile("mF1", "cy8", KFC, fcol(17), EQM, full("ff") + dep(17))
+    tile("mA1", "cyg", KFC, None, EQ, LATE_FF)
+    tile("mA2", "cxn", KFC, None, EQ, LATE_FF)
+    tile("mF1", "cy8", KFC, fcol(17), EQM, LATE_FF + dep(17))
     tile("mF2", "cgh", fcol(19), BIG, EQM, dep(19))
     for h in range(2):
-        ts(T.tal[:, 2 * h:2 * h + 2], T.nv[:, 0:2], A32, fcol(11 + h), (OP.add, OP.mult), full("nv", "ff") + dep(11 + h), [("tal", 2 * h, 2 * h + 2)])
+        ts(T.tal[:, 2 * h:2 * h + 2], T.nv[:, 0:2], A32, fcol(11 + h), (OP.add, OP.mult), full("nv") + LATE_FF + dep(11 + h), [("tal", 2 * h, 2 * h + 2)])
     tt(T.mA[:], T.mA1[:], T.mA2[:], OP.subtract, full("mA1", "mA2"), full("mA"))
     tt(T.mF[:], T.mF1[:], T.mF2[:], OP.add, full("mF1", "mF2"), full("mF"))
     tile("mJ", "c1", T.tau[:, 8:9], None, EQ, full("tau"))
+    mm(T.px[:, 0:P], T.mC[:], T.coord[:], True, True, full("mC", "coord"), full("px"))
+    act(T.ocrd[:], T.px[:, 0:P], ACT.Identity, full("px") + dep(9), full("ocrd"), bias=fcol(9))
     for e in range(2):
         for h in range(2):
             at = 128 * (2 * e + h)
             ts(T.mL[:, at:at + 128], T.c1[:], T.tal[:, 2 * h + e:2 * h + e + 1], None, EQ, full("c1", "tal"), [("mL", at, at + 128)])
-    mm(T.px[:, 0:P], T.mC[:], T.coord[:], True, True, full("mC", "coord"), full("px"))
-    act(T.ocrd[:], T.px[:, 0:P], ACT.Identity, full("px") + dep(9), full("ocrd"), bias=fcol(9))
     for r in range(R):
         fill(T["rq%d" % r][:, KF:KW], 0.0, full("rq%d" % r))
     fill(T.fy[:, KF:KW], 0.0, [("fy", KF, KW)])
@@ -422,12 +437,12 @@ def rank_program(g, core, T, topo):
         ts(T.mQ[:, 128 * u:128 * u + 128], T.c1[:], T.tau[:, u:u + 1], None, EQ, full("c1", "tau"), [("mQ", 128 * u, 128 * u + 128)])
     for h in range(2):
         ts(T.tab[:, 128 * h:128 * h + 128], T.c1[:], 0.0, fcol(10), (OP.is_ge, OP.mult), full("c1") + dep(10), [("tab", 128 * h, 128 * h + 128)])
-    ts(T.tab[:, P:P + KF], T.s4[:], M3, fcol(14), EQM, full("s4", "ff") + dep(14), [("tab", P, P + KF)])
-    answer_places()
+    ts(T.tab[:, P:P + KF], T.s4[:], M3, fcol(14), EQM, full("s4") + LATE_FF + dep(14), [("tab", P, P + KF)])
 
     for r in range(R):
         own(r, 0, EARLY[r])
         foreign(r)
+        answer_places()
         own(r, EARLY[r], S)
         merge(r)
         if r + 1 < R:
@@ -435,11 +450,10 @@ def rank_program(g, core, T, topo):
             mm(T.px[:, 0:P], T.mI[:], T.coord[:], True, False, full("mI", "coord"), full("px"))
             mm(T.px[:, 0:P], T.mI[:], T.gm[:], False, True, full("mI", "gm"), full("px"))
             act(T.pay[:], T.px[:, 0:P], ACT.Identity, full("px"), full("pay"))
-            owners_to_slots(lambda: None)
+            owners_to_slots()
             pack_and_send(r + 1)
             offsets("o", 0)
             offsets("o", 1)
-            answer_places()
         else:
             from_lists("yl", -float(OFF), None, (OP.add,))
             dma("y", "dy", T.y[:], T.yl[:], full("yl"), [], 16)

@@ -6,16 +6,17 @@ ACT = ActivationFunctionType
 N, TT, P, R, S, CAP = 8, 1024, 256, 2, 3, 24
 NO = N - 1
 KF = NO * CAP
-KW = 176
+KW = 192
 OFF = 32
 BIG = 16384.0
 BIGS = 4096.0
 PADL = 4
 TW = TT + 2 * PADL
 NR = CAP // 4
-EARLY = (1, 1)
-HALVES = {"o": ((0, 128, 128, 0, 4), (128, 128, 128, 8, 4)), "f": ((0, 96, 96, 0, 6), (96, 80, 72, 6, 5))}
-SUB = {"o": 2, "f": 1}
+STAGES = (9, 9)
+BETWEEN = (3, 5)
+HALVES = {"o": ((0, 128, 0, 4), (128, 128, 8, 4)), "f": ((0, 96, 0, 3), (96, 80, 6, 3))}
+SUB = 2
 
 SCRATCH = {}
 
@@ -32,33 +33,35 @@ declare("sbuf", [128, 32], "int32", "nbi")
 declare("sbuf", [128, 64], "bfloat16", "nbs")
 declare("sbuf", [128, 32], "float32", "nbf fx w2")
 declare("sbuf", [128, P], "int32", "xi")
-declare("sbuf", [128, P], "bfloat16", "xt coord mask gm pay oy onb osb")
+declare("sbuf", [128, P], "bfloat16", "xt coord mask gm pay onb osb")
+declare("sbuf", [128, P // 16, 16], "bfloat16", "oy")
 declare("sbuf", [128, P], "float32", "ocrd opr")
-declare("sbuf", [128, KW], "bfloat16", "fy fnb fsb rq0 rq1")
+declare("sbuf", [128, KW // 16, 16], "bfloat16", "fy")
+declare("sbuf", [128, KW], "bfloat16", "fnb fsb rq0 rq1")
 declare("sbuf", [128, KW], "float32", "fcrd fpr")
 declare("sbuf", [128, P + 48], "bfloat16", "win0 win1")
 declare("sbuf", [128, 42], "bfloat16", "pk0 pk1")
 declare("sbuf", [128, 16], "int32", "l0 fi ow si sj")
-declare("sbuf", [128, 16], "float32", "l32 ff nv j16 tau oh sl sm yl")
+declare("sbuf", [128, 16], "float32", "l32 ff nv j16 tau sl sm yl")
 declare("sbuf", [128, 4], "float32", "tal")
 declare("sbuf", [128, 16], "uint16", "bc slu of2 oidx fidx")
 declare("sbuf", [128, 32], "bfloat16", "lhl")
-declare("sbuf", [128, 512], "bfloat16", "ex mQ mL")
+declare("sbuf", [128, 512], "bfloat16", "cx mQ mL")
 declare("sbuf", [128, 2], "int32", "ki")
-declare("sbuf", [128, 1], "float32", "k1")
+declare("sbuf", [128, 1], "float32", "k1 k9")
 declare("sbuf", [128, 112], "int32", "qc")
-declare("sbuf", [128, 112], "float32", "d0a d0 sc")
+declare("sbuf", [128, 112], "float32", "d0 sc")
 declare("sbuf", [128, 112], "bfloat16", "oo")
-declare("sbuf", [128, 128], "bfloat16", "c1 cg1 cyg cxg cxn cy8 cgh c4 mA1 mA2 mF1 mF2 mF mI mJ mC mB mU1 mU2 mU3 mU mRH mRL")
+declare("sbuf", [128, 128], "bfloat16", "c1 cp cg1 cyg cxg cxn cy8 cgh c4 mA1 mA2 mF1 mF2 mF mI mP mJ mC mB mU1 mU2 mU3 mRH mRL")
+declare("sbuf", [128, 128], "bfloat16", "dq0 dq1 dq2 dq3")
 declare("sbuf", [128, 128], "float32", "mA w")
 declare("sbuf", [128, 64], "float32", "w1")
-declare("sbuf", [128, KF], "bfloat16", "s4")
+declare("sbuf", [128, KF], "bfloat16", "s4 ds")
 declare("sbuf", [128, P + KF], "bfloat16", "tab send")
 declare("sbuf", [128, 4, 32], "float32", "otr0 otr1")
-declare("sbuf", [128, 6, 32], "float32", "ftr0")
-declare("sbuf", [128, 5, 32], "float32", "ftr1")
-declare("psum", [128, 512], "float32", "pd0 pd1 pp0 pp1 pst px")
-declare("psum", [128, 16, 32], "float32", "pc0 pc1")
+declare("sbuf", [128, 3, 32], "float32", "ftr0 ftr1")
+declare("psum", [128, 512], "float32", "ppf0 ppf1 ppo0 ppo1")
+declare("psum", [128, 16, 32], "float32", "pdf0 pdf1 pdo0 pdo1")
 SEMAPHORES = (["cv", "ct", "cs", "cg", "dl0", "dni", "dxi", "dpl", "dnt", "dnb", "dy"]
               + [s + str(r) for s in ("rqs", "rss", "lq", "lr") for r in range(R)])
 
@@ -136,6 +139,7 @@ def rank_program(g, core, T, topo):
         do("t", lambda e: e.matmul(out, lhsT, rhs, start, stop), reads, writes)
 
     fill(T.xi[:], 0, full("xi"))
+    fill(T.nb[:], 0.0, full("nb"))
     dma("y", "dl0", T.l0[:], T.tet0[:], [], full("l0"), 16)
     dma("s", "dni", T.nbi[:], T.nbr[:], [], full("nbi"), 16)
     hazards("y", [], full("xi"))
@@ -160,20 +164,19 @@ def rank_program(g, core, T, topo):
     iota("c1", T.c1[:], [[1, 128]], 1)
     iota("cg1", T.cg1[:], [[1, 8], [0, 16]], 1)
     iota("nv", T.nv[:], [[1, 16]], 1)
+    iota("cp", T.cp[:], [[1, 16], [16, 8]], 1)
     iota("j16", T.j16[:], [[16, 16]], 0, 1)
     if rank > 0:
         iota("qc", T.qc[:, 0:16 * rank], [[1, rank], [0, 16]], 0, 0, [("qc", 0, 16 * rank)])
     if rank < NO:
         iota("qc", T.qc[:, 16 * rank:112], [[1, NO - rank], [0, 16]], rank + 1, 0, [("qc", 16 * rank, 112)])
-    iota("d0a", T.d0a[:], [[CAP, NO], [0, 16]], P - 1 - int(BIGS))
-    choose("d0", "d0a", [[0, NO], [1, 16]], OP.is_equal, -1000000.0, 0)
+    iota("d0", T.d0[:], [[CAP, NO], [-32768, 16]], P - 1 - int(BIGS))
     iota("cyg", T.cyg[:], [[4, 8], [0, 4], [1, 4]])
     iota("cxg", T.cxg[:], [[4, 8], [1, 4], [0, 4]])
     choose("cxn", "cxg", [[0, 8], [1, 4], [-1, 4]], OP.not_equal, -1.0, 0)
     choose("cy8", "cyg", [[0, 8], [-1, 16]], OP.is_ge, -1.0, 7)
     choose("cgh", "cg1", [[0, 8], [1, 16]], OP.is_ge, -1.0, -8)
     iota("c4", T.c4[:], [[16, 8], [0, 4], [1, 4]], 1)
-    iota("s4", T.s4[:], [[0, KF // 4], [1, 4]])
 
     sh, an = OP.logical_shift_right, OP.bitwise_and
     K16G, K15, KG1, B2, KFC, M3, B3, PAR, A32, XF = [T.ff[:, c:c + 1] for c in range(10)]
@@ -201,31 +204,30 @@ def rank_program(g, core, T, topo):
     columns([(0, an, 112, None, 0), (0, an, 15, None, 0), (1, sh, 4, None, 0), (0, sh, 2, an, 1)], 0)
     tile("mB", "cg1", KG1, None, EQ, EARLY_FF)
     tile("mU1", "c1", T.k1[:], -1.0, (OP.is_lt, OP.mult), full("k1"))
+    tile("mU2", "cg1", KG1, None, (OP.is_lt,), EARLY_FF)
     tile("mU3", "c1", T.k1[:], BIGS, EQM, full("k1"))
-    tt(T.mU2[:], T.mU1[:], T.mB[:], OP.mult, full("mU1", "mB"), full("mU2"))
     ts(T.bc[:, 0:8], T.nv[:, 0:8], 0.0, K15, (OP.mult, OP.add), full("nv") + EARLY_FF, full("bc"))
-    tt(T.mU[:], T.mU2[:], T.mU3[:], OP.add, full("mU2", "mU3"), full("mU"))
-    ts(T.oh[:], T.nv[:], -1.0, K15, (OP.add, OP.is_equal), full("nv") + EARLY_FF, full("oh"))
-    ts(T.w[:, 0:16], T.j16[:], K16G, None, (OP.subtract,), full("j16") + EARLY_FF, [("w", 0, 16)])
+    tile("mP", "cp", T.k1[:], None, EQ, full("k1"))
     tile("mI", "c1", T.k1[:], None, EQ, full("k1"))
-    tile("mRH", "c1", K16G, 9.0, (OP.subtract, OP.is_equal), EARLY_FF)
-    tile("mRL", "c1", K16G, 13.0, (OP.subtract, OP.is_equal), EARLY_FF)
     fill(T.send[:, P:P + KF], 0.0, [("send", P, P + KF)])
 
     def owners_to_slots(*between):
-        todo = list(between) + [lambda: None] * 4
+        todo = list(between) + [lambda: None] * 6
         tt(T.oo[:], T.ow[:].indirect(T.bc[:, 0:NO]), T.qc[:], OP.is_equal, full("ow", "bc", "qc"), full("oo"))
-        mm(T.pst[:, 0:112], T.mB[:], T.oo[:], True, True, full("mB", "oo"), full("pst"))
-        mm(T.pd0[:, 0:112], T.mU[:], T.oo[:], True, True, full("mU", "oo"), full("pd0"))
+        mm(T.ppf0[:, 0:112], T.mB[:], T.oo[:], True, True, full("mB", "oo"), full("ppf0"))
+        for m in (1, 2, 3):
+            mm(T.ppf1[:, 0:112], T["mU%d" % m][:], T.oo[:], m == 1, m == 3, full("mU%d" % m, "oo"), full("ppf1"))
         todo[0]()
-        do("v", lambda e: e.tensor_tensor_scan(T.sc[:], T.d0[:], T.pst[:, 0:112], -1000000.0, OP.max, OP.add), full("d0", "pst"), full("sc"))
+        do("v", lambda e: e.tensor_tensor_scan(T.sc[:], T.d0[:], T.ppf0[:, 0:112], -1000000.0, OP.max, OP.add), full("d0", "ppf0"), full("sc"))
         todo[1]()
-        tt(T.w[:, 16:128], T.pd0[:, 0:112], T.sc[:], OP.add, full("pd0", "sc"), [("w", 16, 128)])
+        tt(T.w[:, 16:128], T.ppf1[:, 0:112], T.sc[:], OP.add, full("ppf1", "sc"), [("w", 16, 128)])
         todo[2]()
         tt(T.w1[:], T.w[:, 0:64], T.w[:, 64:128], OP.max, full("w"), full("w1"))
         todo[3]()
         tt(T.w2[:], T.w1[:, 0:32], T.w1[:, 32:64], OP.max, full("w1"), full("w2"))
+        todo[4]()
         tt(T.sl[:], T.w2[:, 0:16], T.w2[:, 16:32], OP.max, full("w2"), full("sl"))
+        todo[5]()
         copy(T.slu[:], T.sl[:], full("sl"), full("slu"))
 
     def remote(land, sem, lsem, src, at, width, to):
@@ -249,59 +251,71 @@ def rank_program(g, core, T, topo):
 
     def answer_places():
         ts(T.si[:], T.sl[:], 3.0 * P, None, (OP.add,), full("sl"), full("si"))
+        yield
         ts(T.sj[:], T.si[:], 2, None, (OP.arith_shift_right,), full("si"), full("sj"))
+        yield
         tt(T.sm[:], T.sl[:], T.sj[:], OP.min, full("sl", "sj"), full("sm"))
+        yield
         copy(T.of2[:], T.sm[:], full("sm"), full("of2"))
         act(T.mask[:], T.tab[:].indirect(T.slu[:]), ACT.Copy, full("tab", "slu"), full("mask"))
+        yield
 
-    def rows_matmul(p, i, z, zname):
-        at, _, _, _, nb = HALVES[p][i]
-        n = 16 * nb
+    def cols(name, lo, hi):
+        if len(SCRATCH[name][1]) == 2:
+            return T[name][:, lo:hi]
+        return T[name][:, lo // 16:hi // 16, :]
+
+    def rows_matmul(p, i, z):
+        at, _, _, nb = HALVES[p][i]
+        pc, n = "pd%s%d" % (p, i), 16 * nb
         for h in range(2):
-            for e in range(SUB[p]):
+            for e in range(SUB):
                 m = 128 * (2 * e + h)
-                mm(T["pc%d" % i][:, 0:nb, 16 * h:16 * h + 16], T.mL[:, m:m + 128], z[:, at + e * n:at + e * n + n],
-                   e == 0, e == SUB[p] - 1, full("mL") + [(zname, at, at + SUB[p] * n)], full("pc%d" % i))
+                if len(SCRATCH[z][1]) == 2:
+                    src = T[z][:, at + e * n:at + e * n + n]
+                else:
+                    src = T[z][:, at // 16 + e:at // 16 + SUB * nb:SUB, :]
+                mm(T[pc][:, 0:nb, 16 * h:16 * h + 16], T.mL[:, m:m + 128], src,
+                   e == 0, e == SUB - 1, full("mL") + [(z, at, at + SUB * n)], full(pc))
 
     def rows_transpose(p, i):
-        tr, nb = "%str%d" % (p, i), HALVES[p][i][4]
-        do("v", lambda e: e.transpose(T[tr][:], T["pc%d" % i][:, 0:nb, :]), full("pc%d" % i), full(tr))
+        tr, pc, nb = "%str%d" % (p, i), "pd%s%d" % (p, i), HALVES[p][i][3]
+        do("v", lambda e: e.transpose(T[tr][:], T[pc][:, 0:nb, :]), full(pc), full(tr))
 
-    def offsets(p, i):
-        lc, nb = HALVES[p][i][3:5]
+    def offsets(p, i, blocks=True):
+        lc, nb = HALVES[p][i][2:4]
         tr = "%str%d" % (p, i)
-        for e in range(SUB[p]):
-            c = lc + e * nb
-            ts(T[p + "idx"][:, c:c + nb], T[tr][:, :, e], float(PADL - OFF - base), float(TT + PADL), (OP.add, OP.min),
-               full(tr), [(p + "idx", c, c + nb)])
+        for c, n, src in [(lc, SUB * nb, T[tr][:, :, 0:SUB])] if blocks else [(lc + e * nb, nb, T[tr][:, :, e]) for e in range(SUB)]:
+            ts(T[p + "idx"][:, c:c + n], src, float(PADL - OFF - base), float(TT + PADL), (OP.add, OP.min),
+               full(tr), [(p + "idx", c, c + n)])
 
-    def walk(p, i, r, s0, s1):
-        at, kg, k, lc, _ = HALVES[p][i]
-        pd, pp = "pd%d" % i, "pp%d" % i
-        end, gend = at + k, at + kg
+    def walk(p, i, r):
+        at, k, lc, _ = HALVES[p][i]
+        pd, pp = "pd%s%d" % (p, i), "pp%s%d" % (p, i)
+        end = at + k
 
         def reg(name):
-            return [(name, at, gend)]
-        for s in range(s0, s1):
+            return [(name, at, end)]
+        for s in range(S):
             z = ("pay" if p == "o" else "rq%d" % r) if s == 0 else p + "y"
             y = "win%d" % r if p == "o" and s == S - 1 else p + "y"
-            idx = T[p + "idx"][:, lc:lc + kg // 16]
-            idep = [(p + "idx", lc, lc + kg // 16)]
-            tt(T[p + "pr"][:, at:gend], T.pl[:].indirect(idx), T[p + "crd"][:, at:gend], OP.mult, PL + idep + reg(p + "crd"), reg(p + "pr"))
-            act(T[p + "nb"][:, at:gend], T.nb[:].indirect(idx), ACT.Copy, NB + idep, reg(p + "nb"))
-            mm(T[pp][:, 0:k], T.mJ[:], T[z][:, at:end], True, False, full("mJ") + reg(z), full(pp))
+            idx = T[p + "idx"][:, lc:lc + k // 16]
+            idep = [(p + "idx", lc, lc + k // 16)]
+            tt(T[p + "pr"][:, at:end], T.pl[:].indirect(idx), T[p + "crd"][:, at:end], OP.mult, PL + idep + reg(p + "crd"), reg(p + "pr"))
+            act(T[p + "nb"][:, at:end], T.nb[:].indirect(idx), ACT.Copy, NB + idep, reg(p + "nb"))
+            mm(T[pp][:, 0:k], T.mJ[:], cols(z, at, end), True, False, full("mJ") + reg(z), full(pp))
             yield
-            mm(T[pd][:, 0:k], T.mA[:], T[p + "pr"][:, at:end], True, True, full("mA") + reg(p + "pr"), full(pd))
+            mm(T[pd][:, 0:k // 16, 0:16], T.mA[:], T[p + "pr"][:, at:end], True, True, full("mA") + reg(p + "pr"), full(pd))
             yield
-            ts(T[p + "sb"][:, at:end], T[pd][:, 0:k], fcol(7), None, (OP.is_ge,), full(pd) + dep(7), reg(p + "sb"))
+            ts(T[p + "sb"][:, at:end], T[pd][:, 0:k // 16, 0:16], fcol(7), None, (OP.is_ge,), full(pd) + dep(7), reg(p + "sb"))
             yield
             mm(T[pp][:, 0:k], T.mI[:], T[p + "nb"][:, at:end], False, False, full("mI") + reg(p + "nb"), full(pp))
             mm(T[pp][:, 0:k], T.mF[:], T[p + "sb"][:, at:end], False, True, full("mF") + reg(p + "sb"), full(pp))
             yield
-            ts(T[y][:, at:end], T[pp][:, 0:k], fcol(8), 0.0, (OP.add, OP.max), full(pp) + dep(8), [(y, at, end)])
+            ts(cols(y, at, end), T[pp][:, 0:k], fcol(8), 0.0, (OP.add, OP.max), full(pp) + dep(8), [(y, at, end)])
             yield
             if s < S - 1:
-                rows_matmul(p, i, T[y], y)
+                rows_matmul(p, i, y)
                 yield
                 rows_transpose(p, i)
                 yield
@@ -315,49 +329,65 @@ def rank_program(g, core, T, topo):
                 if next(w, 0) == 0:
                     live.remove(w)
 
-    def own(r, s0, s1):
-        weave(*[walk("o", i, r, s0, s1) for i in range(2)])
+    def part(w, n):
+        for _ in range(n):
+            if next(w, 0) == 0:
+                return
+            yield
+
+    owns = {}
+
+    def own(r, n, *more):
+        if r not in owns:
+            owns[r] = [walk("o", i, r) for i in range(2)]
+        weave(*[part(w, n) for w in owns[r]], *more)
 
     def foreign_start(r, i):
         rq = "rq%d" % r
-        at, kg, k, _, _ = HALVES["f"][i]
-        pp = "pp%d" % i
-        rows_matmul("f", i, T[rq], rq)
+        at, k, _, _ = HALVES["f"][i]
+        pp = "ppf%d" % i
+        rows_matmul("f", i, rq)
         yield
-        mm(T[pp][:, 0:kg], T.mC[:], T[rq][:, at:at + kg], True, True, full("mC") + [(rq, at, at + kg)], full(pp))
+        mm(T[pp][:, 0:k], T.mC[:], T[rq][:, at:at + k], True, True, full("mC") + [(rq, at, at + k)], full(pp))
         rows_transpose("f", i)
-        act(T.fcrd[:, at:at + kg], T[pp][:, 0:kg], ACT.Identity, full(pp) + dep(9), [("fcrd", at, at + kg)], bias=fcol(9))
+        act(T.fcrd[:, at:at + k], T[pp][:, 0:k], ACT.Identity, full(pp) + dep(9), [("fcrd", at, at + k)], bias=fcol(9))
         yield
-        offsets("f", i)
+        offsets("f", i, False)
         yield
-        for _ in walk("f", i, r, 0, S):
+        for _ in walk("f", i, r):
             yield
 
     def foreign(r):
         wait("t", "rqs%d" % r, 2 * NO)
-        weave(*[foreign_start(r, i) for i in range(2)])
+        live, n = [foreign_start(r, i) for i in range(2)], 0
+        while live:
+            for w in list(live):
+                if next(w, 0) == 0:
+                    live.remove(w)
+            n += 1
+            if BETWEEN[0] <= n < BETWEEN[1]:
+                own(r, 1)
         pk = "pk%d" % r
         for u in range(4):
-            mm(T.pst[:, 256:298], T.mQ[:, 128 * u:128 * u + 128], T.fy[:, u:KF:4], u == 0, u == 3, full("mQ", "fy"), full("pst"))
-        copy(T[pk][:], T.pst[:, 256:298], full("pst"), full(pk))
+            mm(T.ppf0[:, 256:300], T.mQ[:, 128 * u:128 * u + 128], T.fy[:, 0:11, u:16:4], u == 0, u == 3, full("mQ", "fy"), full("ppf0"))
+        copy(T[pk][:], T.ppf0[:, 256:298], full("ppf0"), full(pk))
         remote("win%d" % r, "rss%d" % r, "lr%d" % r, pk, 0, NR, P)
 
     def merge(r):
         win = "win%d" % r
         wait("v", "rss%d" % r, 2 * NO)
         for i in range(2):
-            at, k, _, lc, _ = HALVES["o"][i]
+            at, k, lc, _ = HALVES["o"][i]
             tt(T.gm[:, at:at + k], T[win][:, 0:P + 42].indirect(T.of2[:, lc:lc + 8]), T.mask[:, at:at + k], OP.mult,
                full(win, "of2", "mask"), [("gm", at, at + k)])
-            rows_matmul("o", i, T.gm, "gm")
+            rows_matmul("o", i, "gm")
         for i in range(2):
             rows_transpose("o", i)
 
     def from_lists(name, s1, s2, ops):
         for i in range(2):
-            for e in range(2):
-                c = HALVES["o"][i][3] + 4 * e
-                tr = "otr%d" % i
+            for e in range(SUB):
+                c, tr = HALVES["o"][i][2] + 4 * e, "otr%d" % i
                 ts(T[name][:, c:c + 4], T[tr][:, :, e], s1, s2, ops, full(tr), [(name, c, c + 4)])
 
     copy(T.lhl[:, 0:16], T.l0[:], full("l0"), [("lhl", 0, 16)])
@@ -365,12 +395,25 @@ def rank_program(g, core, T, topo):
     ts(T.ow[:], T.l0[:], 10, None, (sh,), full("l0"), full("ow"))
     tt(T.lhl[:, 16:32], T.l32[:], T.lhl[:, 0:16], OP.subtract, full("l32") + [("lhl", 0, 16)], [("lhl", 16, 32)])
     for i in range(16):
-        act(T.ex[:, i:512:16], T.lhl[:], ACT.Identity, full("lhl", "oh"), full("ex%d" % i), scale=T.oh[:, i:i + 1])
-    EX = full(*["ex%d" % i for i in range(16)])
+        mm(T.ppo1[0:8, i:512:16], T.mP[:, 8 * i:8 * i + 8], T.lhl[:], True, True, full("mP", "lhl"), full("ppo1"))
+    for h in range(2):
+        act(T.cx[0:8, P * h:P * h + P], T.ppo1[0:8, P * h:P * h + P], ACT.Copy, full("ppo1"), [("cx", P * h, P * h + P)])
 
-    def coordinates():
+    def row_places():
+        ts(T.k9[:], T.k1[:], 16.0, -7.0, (OP.mult, OP.add), full("k1"), full("k9"))
+        for name, b in (("mRH", 0.0), ("mRL", -4.0)):
+            ts(T[name][0:8, :], T.c1[0:8, :], b, T.k9[0:8, :], (OP.add, OP.is_equal), full("c1", "k9"), full(name))
         ts(T.xt[:], T.xi[:], B2, None, (OP.mult,), XI + EARLY_FF, full("xt"))
-        tt(T.coord[:], T.xi[:], T.xt[:], OP.subtract, XI + full("xt"), full("coord"))
+
+    def low(lo, hi):
+        tt(T.coord[:, lo:hi], T.xi[:, lo:hi], T.xt[:, lo:hi], OP.subtract, XI + full("xt"), [("coord", lo, hi)])
+
+    def low0():
+        low(0, P // 2)
+
+    def low1():
+        ts(T.w[:, 0:16], T.j16[:], K16G, None, (OP.subtract,), full("j16") + EARLY_FF, [("w", 0, 16)])
+        low(P // 2, P)
 
     def codes0():
         copy(T.nbs[:, 0:32], T.nbi[:], full("nbi"), [("nbs", 0, 32)])
@@ -383,22 +426,22 @@ def rank_program(g, core, T, topo):
         for h in range(2):
             dma("y", "dnt", T.nbt[128 * h:128 * h + 128, :], T.nbs[:, 32 * h:32 * h + 32], full("nbs"), full("nbt%d" % h), 32)
 
-    owners_to_slots(coordinates, codes0, codes1, codes2)
-    mm(T.px[:, 0:P], T.mI[:], T.coord[:], True, False, full("mI", "coord"), full("px"))
-    mm(T.px[:, 0:P], T.mRH[:], T.ex[:, 0:P], False, False, full("mRH") + EX, full("px"))
-    mm(T.px[:, 0:P], T.mRL[:], T.ex[:, P:2 * P], False, True, full("mRL") + EX, full("px"))
-    act(T.pay[:], T.px[:, 0:P], ACT.Identity, full("px"), full("pay"))
+    owners_to_slots(row_places, low0, low1, codes0, codes1, codes2)
+    mm(T.ppo0[:, 0:P], T.mI[:], T.coord[:], True, False, full("mI", "coord"), full("ppo0"))
+    mm(T.ppo0[:, 0:P], T.mRH[0:8, :], T.cx[0:8, 0:P], False, False, full("mRH") + [("cx", 0, P)], full("ppo0"))
+    mm(T.ppo0[:, 0:P], T.mRL[0:8, :], T.cx[0:8, P:2 * P], False, True, full("mRL") + [("cx", P, 2 * P)], full("ppo0"))
+    act(T.pay[:], T.ppo0[:, 0:P], ACT.Identity, full("ppo0"), full("pay"))
     pack_and_send(0)
 
-    fill(T.nb[:], 0.0, full("nb"))
+    iota("s4", T.s4[:], [[0, KF // 4], [1, 4]])
     hazards("y", full("nb"), [])
     for k in range(8):
         dma("y", "dnb", T.nb[16 * k:16 * k + 8, PADL:PADL + TT], T.nbt[:], full("nbt0", "nbt1"), full("nb%d" % k), 128)
     NB = full("nb", *["nb%d" % k for k in range(8)])
-    fill(T.pl[:, 0:PADL], 0, [("pl", 0, PADL)])
-    fill(T.pl[:, TT + PADL:TW], 0, [("pl", TT + PADL, TW)])
     columns([(0, sh, 2, None, 0), (0, an, 3, None, 0), (0, sh, 3, an, 1), (0, sh, 4, an, 1), (0, an, 96, None, 0),
              (0, sh, 2, an, 3)], 4)
+    fill(T.pl[:, 0:PADL], 0, [("pl", 0, PADL)])
+    fill(T.pl[:, TT + PADL:TW], 0, [("pl", TT + PADL, TW)])
     ts(T.oidx[:], T.l0[:], float(PADL - base), float(TT + PADL), (OP.add, OP.min), full("l0"), full("oidx"))
     fx(13, B2, 4.0, K16G, OP.mult, OP.add)
     fx(14, B3, -1.0, 1.0, OP.mult, OP.add)
@@ -424,36 +467,40 @@ def rank_program(g, core, T, topo):
     tt(T.mA[:], T.mA1[:], T.mA2[:], OP.subtract, full("mA1", "mA2"), full("mA"))
     tt(T.mF[:], T.mF1[:], T.mF2[:], OP.add, full("mF1", "mF2"), full("mF"))
     tile("mJ", "c1", T.tau[:, 8:9], None, EQ, full("tau"))
-    mm(T.px[:, 0:P], T.mC[:], T.coord[:], True, True, full("mC", "coord"), full("px"))
-    act(T.ocrd[:], T.px[:, 0:P], ACT.Identity, full("px") + dep(9), full("ocrd"), bias=fcol(9))
+    mm(T.ppo0[:, 0:P], T.mC[:], T.coord[:], True, True, full("mC", "coord"), full("ppo0"))
+    act(T.ocrd[:], T.ppo0[:, 0:P], ACT.Identity, full("ppo0") + dep(9), full("ocrd"), bias=fcol(9))
     for e in range(2):
         for h in range(2):
             at = 128 * (2 * e + h)
             ts(T.mL[:, at:at + 128], T.c1[:], T.tal[:, 2 * h + e:2 * h + e + 1], None, EQ, full("c1", "tal"), [("mL", at, at + 128)])
     for r in range(R):
         fill(T["rq%d" % r][:, KF:KW], 0.0, full("rq%d" % r))
-    fill(T.fy[:, KF:KW], 0.0, [("fy", KF, KW)])
+    fill(cols("fy", 176, KW), 0.0, [("fy", 176, KW)])
+    act(T.tab[:, 0:P], T.pay[:], ACT.Identity, full("pay") + dep(10), [("tab", 0, P)], scale=0.0, bias=fcol(10))
+    act(T.ds[:], T.s4[:], ACT.Abs, full("s4") + LATE_FF, full("ds"), scale=-1.0, bias=M3)
     for u in range(4):
-        ts(T.mQ[:, 128 * u:128 * u + 128], T.c1[:], T.tau[:, u:u + 1], None, EQ, full("c1", "tau"), [("mQ", 128 * u, 128 * u + 128)])
-    for h in range(2):
-        ts(T.tab[:, 128 * h:128 * h + 128], T.c1[:], 0.0, fcol(10), (OP.is_ge, OP.mult), full("c1") + dep(10), [("tab", 128 * h, 128 * h + 128)])
-    ts(T.tab[:, P:P + KF], T.s4[:], M3, fcol(14), EQM, full("s4") + LATE_FF + dep(14), [("tab", P, P + KF)])
+        act(T["dq%d" % u][:], T.c1[:], ACT.Abs, full("c1", "tau"), full("dq%d" % u), scale=-1.0, bias=T.tau[:, u:u + 1])
+    act(T.tab[:, P:P + KF], T.ds[:], ACT.Relu, full("ds") + dep(14), [("tab", P, P + KF)], scale=-1.0, bias=fcol(14))
+
+    def answer_matrices():
+        for u in range(4):
+            act(T.mQ[:, 128 * u:128 * u + 128], T["dq%d" % u][:], ACT.Relu, full("dq%d" % u), [("mQ", 128 * u, 128 * u + 128)], scale=-1.0, bias=1.0)
+            yield
 
     for r in range(R):
-        own(r, 0, EARLY[r])
+        own(r, STAGES[r], answer_places(), *([answer_matrices()] if r == 0 else []))
         foreign(r)
-        answer_places()
-        own(r, EARLY[r], S)
+        own(r, 8 * S)
         merge(r)
         if r + 1 < R:
             from_lists("ow", 1.0 / TT, -(OFF + 511.5) / TT, (OP.mult, OP.add))
-            mm(T.px[:, 0:P], T.mI[:], T.coord[:], True, False, full("mI", "coord"), full("px"))
-            mm(T.px[:, 0:P], T.mI[:], T.gm[:], False, True, full("mI", "gm"), full("px"))
-            act(T.pay[:], T.px[:, 0:P], ACT.Identity, full("px"), full("pay"))
+            mm(T.ppo0[:, 0:P], T.mI[:], T.coord[:], True, False, full("mI", "coord"), full("ppo0"))
+            mm(T.ppo0[:, 0:P], T.mI[:], T.gm[:], False, True, full("mI", "gm"), full("ppo0"))
+            act(T.pay[:], T.ppo0[:, 0:P], ACT.Identity, full("ppo0"), full("pay"))
             owners_to_slots()
             pack_and_send(r + 1)
-            offsets("o", 0)
-            offsets("o", 1)
+            offsets("o", 0, False)
+            offsets("o", 1, False)
         else:
             from_lists("yl", -float(OFF), None, (OP.add,))
             dma("y", "dy", T.y[:], T.yl[:], full("yl"), [], 16)

@@ -9,12 +9,12 @@ KF = NO * CAP
 KW = 192
 OFF = 32
 BIG = 16384.0
-BIGS = 4096.0
+BIGS = 2048.0
 PADL = 4
 TW = TT + 2 * PADL
 NR = CAP // 4
-STAGES = (9, 9)
-BETWEEN = (3, 5)
+STAGES = (5, 9)
+BETWEEN = ((3, 4, 7, 8, 9, 12, 17, 20), (3, 5, 11, 12, 20))
 HALVES = {"o": ((0, 128, 0, 4), (128, 128, 8, 4)), "f": ((0, 96, 0, 3), (96, 80, 6, 3))}
 SUB = 2
 
@@ -31,7 +31,7 @@ declare("sbuf", [128, TW], "bfloat16", "nb")
 declare("dram", [256, 32], "bfloat16", "nbt")
 declare("sbuf", [128, 32], "int32", "nbi")
 declare("sbuf", [128, 64], "bfloat16", "nbs")
-declare("sbuf", [128, 32], "float32", "nbf fx w2")
+declare("sbuf", [128, 32], "float32", "nbf fx")
 declare("sbuf", [128, P], "int32", "xi")
 declare("sbuf", [128, P], "bfloat16", "xt coord mask gm pay onb osb")
 declare("sbuf", [128, P // 16, 16], "bfloat16", "oy")
@@ -50,12 +50,12 @@ declare("sbuf", [128, 512], "bfloat16", "cx mQ mL")
 declare("sbuf", [128, 2], "int32", "ki")
 declare("sbuf", [128, 1], "float32", "k1 k9")
 declare("sbuf", [128, 112], "int32", "qc")
-declare("sbuf", [128, 112], "float32", "d0 sc")
-declare("sbuf", [128, 112], "bfloat16", "oo")
-declare("sbuf", [128, 128], "bfloat16", "c1 cp cg1 cyg cxg cxn cy8 cgh c4 mA1 mA2 mF1 mF2 mF mI mP mJ mC mB mU1 mU2 mU3 mRH mRL")
+declare("sbuf", [128, 112], "float32", "d0")
+declare("sbuf", [128, 112], "bfloat16", "oo sc")
+declare("sbuf", [128, 128], "bfloat16", "c1 cp cg1 cyg cxg cxn cy8 cgh c4 ct")
+declare("sbuf", [128, 128], "bfloat16", "mA1 mA2 mF1 mF2 mF mI mP mJ mC mB mU1 mU2 mU3 mU mRH mRL")
 declare("sbuf", [128, 128], "bfloat16", "dq0 dq1 dq2 dq3")
-declare("sbuf", [128, 128], "float32", "mA w")
-declare("sbuf", [128, 64], "float32", "w1")
+declare("sbuf", [128, 128], "float32", "mA dd sx")
 declare("sbuf", [128, KF], "bfloat16", "s4 ds")
 declare("sbuf", [128, P + KF], "bfloat16", "tab send")
 declare("sbuf", [128, 4, 32], "float32", "otr0 otr1")
@@ -139,7 +139,6 @@ def rank_program(g, core, T, topo):
         do("t", lambda e: e.matmul(out, lhsT, rhs, start, stop), reads, writes)
 
     fill(T.xi[:], 0, full("xi"))
-    fill(T.nb[:], 0.0, full("nb"))
     dma("y", "dl0", T.l0[:], T.tet0[:], [], full("l0"), 16)
     dma("s", "dni", T.nbi[:], T.nbr[:], [], full("nbi"), 16)
     hazards("y", [], full("xi"))
@@ -164,13 +163,15 @@ def rank_program(g, core, T, topo):
     iota("c1", T.c1[:], [[1, 128]], 1)
     iota("cg1", T.cg1[:], [[1, 8], [0, 16]], 1)
     iota("nv", T.nv[:], [[1, 16]], 1)
-    iota("cp", T.cp[:], [[1, 16], [16, 8]], 1)
-    iota("j16", T.j16[:], [[16, 16]], 0, 1)
+    iota("j16", T.j16[:], [[16, 16]], 1, 1)
+    iota("ct", T.ct[:], [[0, 16], [CAP, 8]], P - int(BIGS))
     if rank > 0:
         iota("qc", T.qc[:, 0:16 * rank], [[1, rank], [0, 16]], 0, 0, [("qc", 0, 16 * rank)])
     if rank < NO:
         iota("qc", T.qc[:, 16 * rank:112], [[1, NO - rank], [0, 16]], rank + 1, 0, [("qc", 16 * rank, 112)])
-    iota("d0", T.d0[:], [[CAP, NO], [-32768, 16]], P - 1 - int(BIGS))
+    iota("cp", T.cp[:], [[1, 16], [16, 8]], 1)
+    iota("d0", T.d0[:], [[0, NO], [1000, 16]])
+    iota("dd", T.dd[:], [[0, 16], [4000, 8]])
     iota("cyg", T.cyg[:], [[4, 8], [0, 4], [1, 4]])
     iota("cxg", T.cxg[:], [[4, 8], [1, 4], [0, 4]])
     choose("cxn", "cxg", [[0, 8], [1, 4], [-1, 4]], OP.not_equal, -1.0, 0)
@@ -182,9 +183,10 @@ def rank_program(g, core, T, topo):
     K16G, K15, KG1, B2, KFC, M3, B3, PAR, A32, XF = [T.ff[:, c:c + 1] for c in range(10)]
     EARLY_FF, LATE_FF = [("ff", 0, 4)], [("ff", 4, 10)]
 
-    def columns(ints, at):
+    def columns(ints, at, between=lambda: None):
         for c, (src, o0, n0, o1, n1) in enumerate(ints):
             ts(T.fi[:, at + c:at + c + 1], T.ki[:, src:src + 1], n0, None if o1 is None else n1, (o0, o1), full("ki"), [("fi", at + c, at + c + 1)])
+        between()
         end = at + len(ints)
         copy(T.ff[:, at:end], T.fi[:, at:end], [("fi", at, end)], [("ff", at, end)])
 
@@ -201,34 +203,39 @@ def rank_program(g, core, T, topo):
         ts(T[name][:], T[src][:], col, s2, ops, full(src) + reads, full(name))
 
     EQ, EQM = (OP.is_equal,), (OP.is_equal, OP.mult)
-    columns([(0, an, 112, None, 0), (0, an, 15, None, 0), (1, sh, 4, None, 0), (0, sh, 2, an, 1)], 0)
-    tile("mB", "cg1", KG1, None, EQ, EARLY_FF)
-    tile("mU1", "c1", T.k1[:], -1.0, (OP.is_lt, OP.mult), full("k1"))
-    tile("mU2", "cg1", KG1, None, (OP.is_lt,), EARLY_FF)
-    tile("mU3", "c1", T.k1[:], BIGS, EQM, full("k1"))
-    ts(T.bc[:, 0:8], T.nv[:, 0:8], 0.0, K15, (OP.mult, OP.add), full("nv") + EARLY_FF, full("bc"))
-    tile("mP", "cp", T.k1[:], None, EQ, full("k1"))
+    columns([(0, an, 112, None, 0), (0, an, 15, None, 0), (1, sh, 4, None, 0), (0, sh, 2, an, 1)], 0,
+            lambda: fill(T.nb[:], 0.0, full("nb")))
     tile("mI", "c1", T.k1[:], None, EQ, full("k1"))
+    tile("mU1", "c1", T.k1[:], -1.0, (OP.is_lt, OP.mult), full("k1"))
+    tile("mU3", "c1", T.k1[:], BIGS, EQM, full("k1"))
+    tile("mU2", "cg1", KG1, None, (OP.is_lt,), EARLY_FF)
+    for m in (1, 3, 2):
+        mm(T.ppo0[:, 0:128], T.mI[:], T["mU%d" % m][:], m == 1, m == 2, full("mI", "mU%d" % m), full("ppo0"))
+    act(T.mU[:], T.ppo0[:, 0:128], ACT.Copy, full("ppo0"), full("mU"))
+    tile("mB", "cg1", KG1, None, EQ, EARLY_FF)
+    ts(T.bc[:, 0:8], T.nv[:, 0:8], 0.0, K15, (OP.mult, OP.add), full("nv") + EARLY_FF, full("bc"))
+    ts(T.k9[:], T.k1[:], 16.0, -7.0, (OP.mult, OP.add), full("k1"), full("k9"))
+    for name, b in (("mRH", 0.0), ("mRL", -4.0)):
+        ts(T[name][0:8, :], T.c1[0:8, :], b, T.k9[0:8, :], (OP.add, OP.is_equal), full("c1", "k9"), full(name))
+    ts(T.ct[:, 7:128:8], T.j16[:], K16G, None, (OP.subtract,), full("j16", "ct") + EARLY_FF, full("ct"))
     fill(T.send[:, P:P + KF], 0.0, [("send", P, P + KF)])
 
     def owners_to_slots(*between):
-        todo = list(between) + [lambda: None] * 6
+        todo = list(between) + [lambda: None] * 4
         tt(T.oo[:], T.ow[:].indirect(T.bc[:, 0:NO]), T.qc[:], OP.is_equal, full("ow", "bc", "qc"), full("oo"))
         mm(T.ppf0[:, 0:112], T.mB[:], T.oo[:], True, True, full("mB", "oo"), full("ppf0"))
-        for m in (1, 2, 3):
-            mm(T.ppf1[:, 0:112], T["mU%d" % m][:], T.oo[:], m == 1, m == 3, full("mU%d" % m, "oo"), full("ppf1"))
+        mm(T.ppf1[:, 0:128], T.mI[:], T.ct[:], True, False, full("mI", "ct"), full("ppf1"))
+        for d in range(NO):
+            mm(T.ppf1[:, d:128:8], T.mU[:], T.oo[:, 16 * d:16 * d + 16], False, False, full("mU", "oo"), full("ppf1"))
         todo[0]()
-        do("v", lambda e: e.tensor_tensor_scan(T.sc[:], T.d0[:], T.ppf0[:, 0:112], -1000000.0, OP.max, OP.add), full("d0", "ppf0"), full("sc"))
+        do("v", lambda e: e.tensor_tensor_scan(T.sc[:], T.d0[:], T.ppf0[:, 0:112], 0.0, OP.min, OP.add), full("d0", "ppf0"), full("sc"))
         todo[1]()
-        tt(T.w[:, 16:128], T.ppf1[:, 0:112], T.sc[:], OP.add, full("ppf1", "sc"), [("w", 16, 128)])
+        for d in range(NO):
+            mm(T.ppf1[:, d:128:8], T.mI[:], T.sc[:, 16 * d:16 * d + 16], False, d == NO - 1, full("mI", "sc"), full("ppf1"))
+        do("v", lambda e: e.tensor_tensor_scan(T.sx[:], T.dd[:], T.ppf1[:, 0:128], 0.0, OP.min, OP.max), full("dd", "ppf1"), full("sx"))
         todo[2]()
-        tt(T.w1[:], T.w[:, 0:64], T.w[:, 64:128], OP.max, full("w"), full("w1"))
+        ts(T.slu[:], T.sx[:, 7:128:8], -1.0, None, (OP.add,), full("sx"), full("slu"))
         todo[3]()
-        tt(T.w2[:], T.w1[:, 0:32], T.w1[:, 32:64], OP.max, full("w1"), full("w2"))
-        todo[4]()
-        tt(T.sl[:], T.w2[:, 0:16], T.w2[:, 16:32], OP.max, full("w2"), full("sl"))
-        todo[5]()
-        copy(T.slu[:], T.sl[:], full("sl"), full("slu"))
 
     def remote(land, sem, lsem, src, at, width, to):
         hazards("g", full(src), [])
@@ -250,7 +257,8 @@ def rank_program(g, core, T, topo):
         remote("rq%d" % r, "rqs%d" % r, "lq%d" % r, "send", P, CAP, 0)
 
     def answer_places():
-        ts(T.si[:], T.sl[:], 3.0 * P, None, (OP.add,), full("sl"), full("si"))
+        ts(T.sl[:], T.sx[:, 7:128:8], -1.0, None, (OP.add,), full("sx"), full("sl"))
+        ts(T.si[:], T.sx[:, 7:128:8], 3.0 * P - 1.0, None, (OP.add,), full("sx"), full("si"))
         yield
         ts(T.sj[:], T.si[:], 2, None, (OP.arith_shift_right,), full("si"), full("sj"))
         yield
@@ -365,7 +373,7 @@ def rank_program(g, core, T, topo):
                 if next(w, 0) == 0:
                     live.remove(w)
             n += 1
-            if BETWEEN[0] <= n < BETWEEN[1]:
+            if n in BETWEEN[r]:
                 own(r, 1)
         pk = "pk%d" % r
         for u in range(4):
@@ -384,49 +392,38 @@ def rank_program(g, core, T, topo):
         for i in range(2):
             rows_transpose("o", i)
 
-    def from_lists(name, s1, s2, ops):
+    def list_parts():
         for i in range(2):
             for e in range(SUB):
-                c, tr = HALVES["o"][i][2] + 4 * e, "otr%d" % i
-                ts(T[name][:, c:c + 4], T[tr][:, :, e], s1, s2, ops, full(tr), [(name, c, c + 4)])
+                yield i, T["otr%d" % i][:, :, e], HALVES["o"][i][2] + 4 * e
 
     copy(T.lhl[:, 0:16], T.l0[:], full("l0"), [("lhl", 0, 16)])
     ts(T.l32[:], T.l0[:], float(OFF), None, (OP.add,), full("l0"), full("l32"))
     ts(T.ow[:], T.l0[:], 10, None, (sh,), full("l0"), full("ow"))
     tt(T.lhl[:, 16:32], T.l32[:], T.lhl[:, 0:16], OP.subtract, full("l32") + [("lhl", 0, 16)], [("lhl", 16, 32)])
+    tile("mP", "cp", T.k1[:], None, EQ, full("k1"))
     for i in range(16):
         mm(T.ppo1[0:8, i:512:16], T.mP[:, 8 * i:8 * i + 8], T.lhl[:], True, True, full("mP", "lhl"), full("ppo1"))
     for h in range(2):
         act(T.cx[0:8, P * h:P * h + P], T.ppo1[0:8, P * h:P * h + P], ACT.Copy, full("ppo1"), [("cx", P * h, P * h + P)])
 
-    def row_places():
-        ts(T.k9[:], T.k1[:], 16.0, -7.0, (OP.mult, OP.add), full("k1"), full("k9"))
-        for name, b in (("mRH", 0.0), ("mRL", -4.0)):
-            ts(T[name][0:8, :], T.c1[0:8, :], b, T.k9[0:8, :], (OP.add, OP.is_equal), full("c1", "k9"), full(name))
+    def high():
         ts(T.xt[:], T.xi[:], B2, None, (OP.mult,), XI + EARLY_FF, full("xt"))
 
-    def low(lo, hi):
-        tt(T.coord[:, lo:hi], T.xi[:, lo:hi], T.xt[:, lo:hi], OP.subtract, XI + full("xt"), [("coord", lo, hi)])
-
-    def low0():
-        low(0, P // 2)
-
-    def low1():
-        ts(T.w[:, 0:16], T.j16[:], K16G, None, (OP.subtract,), full("j16") + EARLY_FF, [("w", 0, 16)])
-        low(P // 2, P)
+    def lows():
+        for lo, hi in ((0, P // 2), (P // 2, P)):
+            tt(T.coord[:, lo:hi], T.xi[:, lo:hi], T.xt[:, lo:hi], OP.subtract, XI + full("xt"), [("coord", lo, hi)])
 
     def codes0():
         copy(T.nbs[:, 0:32], T.nbi[:], full("nbi"), [("nbs", 0, 32)])
 
     def codes1():
         ts(T.nbf[:], T.nbi[:], float(OFF), None, (OP.add,), full("nbi"), full("nbf"))
-
-    def codes2():
         tt(T.nbs[:, 32:64], T.nbf[:], T.nbs[:, 0:32], OP.subtract, full("nbf") + [("nbs", 0, 32)], [("nbs", 32, 64)])
         for h in range(2):
             dma("y", "dnt", T.nbt[128 * h:128 * h + 128, :], T.nbs[:, 32 * h:32 * h + 32], full("nbs"), full("nbt%d" % h), 32)
 
-    owners_to_slots(row_places, low0, low1, codes0, codes1, codes2)
+    owners_to_slots(high, lows, codes0, codes1)
     mm(T.ppo0[:, 0:P], T.mI[:], T.coord[:], True, False, full("mI", "coord"), full("ppo0"))
     mm(T.ppo0[:, 0:P], T.mRH[0:8, :], T.cx[0:8, 0:P], False, False, full("mRH") + [("cx", 0, P)], full("ppo0"))
     mm(T.ppo0[:, 0:P], T.mRL[0:8, :], T.cx[0:8, P:2 * P], False, True, full("mRL") + [("cx", P, 2 * P)], full("ppo0"))
@@ -493,7 +490,8 @@ def rank_program(g, core, T, topo):
         own(r, 8 * S)
         merge(r)
         if r + 1 < R:
-            from_lists("ow", 1.0 / TT, -(OFF + 511.5) / TT, (OP.mult, OP.add))
+            for i, src, c in list_parts():
+                ts(T.ow[:, c:c + 4], src, 1.0 / TT, -(OFF + 511.5) / TT, (OP.mult, OP.add), full("otr%d" % i), [("ow", c, c + 4)])
             mm(T.ppo0[:, 0:P], T.mI[:], T.coord[:], True, False, full("mI", "coord"), full("ppo0"))
             mm(T.ppo0[:, 0:P], T.mI[:], T.gm[:], False, True, full("mI", "gm"), full("ppo0"))
             act(T.pay[:], T.ppo0[:, 0:P], ACT.Identity, full("ppo0"), full("pay"))
@@ -502,7 +500,8 @@ def rank_program(g, core, T, topo):
             offsets("o", 0, False)
             offsets("o", 1, False)
         else:
-            from_lists("yl", -float(OFF), None, (OP.add,))
+            for i, src, c in list_parts():
+                ts(T.yl[:, c:c + 4], src, -float(OFF), None, (OP.add,), full("otr%d" % i), [("yl", c, c + 4)])
             dma("y", "dy", T.y[:], T.yl[:], full("yl"), [], 16)
     for sem in ("ct", "cs", "cg"):
         wait("g", sem, count[sem])

from concourse.bass import DstId, RemoteDMATransfer
from concourse.mybir import AluOpType, ActivationFunctionType

OP = AluOpType
ACT = ActivationFunctionType
N, TT, P, R, S, CAP = 8, 1024, 256, 2, 3, 24
NO = N - 1
KF = NO * CAP
KW = 192
OFF = 32
BIG = 16384.0
BIGS = 2048.0
PADL = 4
TW = TT + 2 * PADL
NR = CAP // 4
STAGES = (5, 9)
BETWEEN = ((3, 4, 7, 8, 9, 12, 17, 20), (3, 5, 11, 12, 20))
HALVES = {"o": ((0, 128, 0, 4), (128, 128, 8, 4)), "f": ((0, 96, 0, 3), (96, 80, 6, 3))}
SUB = 2

SCRATCH = {}


def declare(where, shape, dtype, names):
    for n in names.split():
        SCRATCH[n] = (where, shape, dtype)


declare("sbuf", [128, TW], "int32", "pl")
declare("sbuf", [128, TW], "bfloat16", "nb")
declare("dram", [256, 32], "bfloat16", "nbt")
declare("sbuf", [128, 32], "int32", "nbi")
declare("sbuf", [128, 64], "bfloat16", "nbs")
declare("sbuf", [128, 32], "float32", "nbf fx")
declare("sbuf", [128, P], "int32", "xi")
declare("sbuf", [128, P], "bfloat16", "xt coord mask gm pay onb osb")
declare("sbuf", [128, P // 16, 16], "bfloat16", "oy")
declare("sbuf", [128, P], "float32", "ocrd opr")
declare("sbuf", [128, KW // 16, 16], "bfloat16", "fy")
declare("sbuf", [128, KW], "bfloat16", "fnb fsb rq0 rq1")
declare("sbuf", [128, KW], "float32", "fcrd fpr")
declare("sbuf", [128, P + 48], "bfloat16", "win0 win1")
declare("sbuf", [128, 42], "bfloat16", "pk0 pk1")
declare("sbuf", [128, 16], "int32", "l0 fi ow si sj")
declare("sbuf", [128, 16], "float32", "l32 ff nv j16 tau sl sm yl")
declare("sbuf", [128, 4], "float32", "tal")
declare("sbuf", [128, 16], "uint16", "bc slu of2 oidx fidx")
declare("sbuf", [128, 32], "bfloat16", "lhl")
declare("sbuf", [128, 512], "bfloat16", "cx mQ mL")
declare("sbuf", [128, 2], "int32", "ki")
declare("sbuf", [128, 1], "float32", "k1 k9")
declare("sbuf", [128, 112], "int32", "qc")
declare("sbuf", [128, 112], "float32", "d0")
declare("sbuf", [128, 112], "bfloat16", "oo sc")
declare("sbuf", [128, 128], "bfloat16", "c1 cp cg1 cyg cxg cxn cy8 cgh c4 ct")
declare("sbuf", [128, 128], "bfloat16", "mA1 mA2 mF1 mF2 mF mI mP mJ mC mB mU1 mU2 mU3 mU mRH mRL")
declare("sbuf", [128, 128], "bfloat16", "dq0 dq1 dq2 dq3")
declare("sbuf", [128, 128], "float32", "mA dd sx")
declare("sbuf", [128, KF], "bfloat16", "s4 ds")
declare("sbuf", [128, P + KF], "bfloat16", "tab send")
declare("sbuf", [128, 4, 32], "float32", "otr0 otr1")
declare("sbuf", [128, 3, 32], "float32", "ftr0 ftr1")
declare("psum", [128, 512], "float32", "ppf0 ppf1 ppo0 ppo1")
declare("psum", [128, 16, 32], "float32", "pdf0 pdf1 pdo0 pdo1")
SEMAPHORES = (["cv", "ct", "cs", "cg", "dl0", "dni", "dxi", "dpl", "dnt", "dnb", "dy"]
              + [s + str(r) for s in ("rqs", "rss", "lq", "lr") for r in range(R)])


def rank_program(g, core, T, topo):
    rank = T.rank_of(core)
    if rank is None:
        return
    base = rank * TT
    others = [q for q in range(N) if q != rank]
    queue = {"v": g.vector, "t": g.tensor, "s": g.scalar, "g": g, "y": g.sync}
    own_sem = {"v": "cv", "t": "ct", "s": "cs", "g": "cg"}
    count, waited, acc = {}, {}, {}

    def wait(q, sem, val):
        if waited.get((q, sem), 0) < val:
            queue[q].wait_ge(T.sem[sem], val)
            waited[(q, sem)] = val

    def hazards(q, reads, writes):
        need = {}
        for kind, regs in (("r", reads), ("w", writes)):
            for b, lo, hi in regs:
                for l2, h2, k2, q2, sem, val in acc.get(b, []):
                    if l2 < hi and lo < h2 and (kind == "w" or k2 == "w"):
                        if q == "t" and q2 == "t" and k2 == "w" and kind == "w":
                            continue
                        need[sem] = max(need.get(sem, 0), val)
        for sem in need:
            wait(q, sem, need[sem])

    def note(q, reads, writes, sem, val):
        for kind, regs in (("r", reads), ("w", writes)):
            for b, lo, hi in regs:
                old = acc.get(b, [])
                if kind == "w":
                    old = [a for a in old if not (lo <= a[0] and a[1] <= hi)]
                acc[b] = old + [(lo, hi, kind, q, sem, val)]

    def do(q, fn, reads, writes):
        hazards(q, reads, writes)
        sem = own_sem[q]
        count[sem] = count.get(sem, 0) + 1
        fn(queue[q]).then_inc(T.sem[sem], 1)
        note(q, reads, writes, sem, count[sem])

    def full(*names):
        return [(n, 0, 1 << 20) for n in names]

    def dma(q, sem, out, in_, reads, writes, total):
        hazards(q, reads, writes)
        queue[q].dma_start(out, in_).then_inc(T.sem[sem], 16)
        count[sem] = count.get(sem, 0) + 16
        note("d", reads, writes, sem, total)

    def ts(out, in0, s1, s2, ops, reads, writes):
        if s2 is None:
            do("v", lambda e: e.tensor_scalar(out, in0, s1, None, ops[0]), reads, writes)
        else:
            do("v", lambda e: e.tensor_scalar(out, in0, s1, s2, ops[0], ops[1]), reads, writes)

    def tt(out, a, b, op, reads, writes):
        do("v", lambda e: e.tensor_tensor(out, a, b, op), reads, writes)

    def copy(out, in_, reads, writes):
        do("v", lambda e: e.tensor_copy(out, in_), reads, writes)

    def fill(ap, c, writes):
        do("v", lambda e: e.memset(ap, c), [], writes)

    def act(out, in_, func, reads, writes, **kw):
        do("s", lambda e: e.activation(out, in_, func, **kw), reads, writes)

    def mm(out, lhsT, rhs, start, stop, reads, writes):
        do("t", lambda e: e.matmul(out, lhsT, rhs, start, stop), reads, writes)

    fill(T.xi[:], 0, full("xi"))
    dma("y", "dl0", T.l0[:], T.tet0[:], [], full("l0"), 16)
    dma("s", "dni", T.nbi[:], T.nbr[:], [], full("nbi"), 16)
    hazards("y", [], full("xi"))
    hazards("s", [], full("xi"))
    for c in range(3):
        for h, q in ((9, "y"), (13, "s")):
            dma(q, "dxi", T.xi[h + c:128:16, :], T.pts[c:24:3, :], [], full("xi%d" % (h + c)), 96)
    XI = full("xi", *["xi%d" % h for h in (9, 10, 11, 13, 14, 15)])
    for k in range(8):
        dma("ys"[k % 2], "dpl", T.pl[16 * k:16 * k + 16, PADL:PADL + TT], T.planes[:], [], full("pl%d" % k), 128)
    PL = full("pl", *["pl%d" % k for k in range(8)])

    def iota(name, ap, pattern, b=0, ch=0, reg=None):
        kw = {} if SCRATCH[name][2] == "int32" else {"allow_small_or_imprecise_dtypes": True}
        do("g", lambda e: e.iota(ap, pattern, b, ch, **kw), [], reg or full(name))

    def choose(name, src, pattern, cmp, fill_, b):
        do("g", lambda e: e.affine_select(T[name][:], T[src][:], pattern, cmp, fill_, b, 0), full(src), full(name))

    iota("ki", T.ki[:], [[16, 2]], 0, 1)
    iota("k1", T.k1[:], [[0, 1]], 1, 1)
    iota("c1", T.c1[:], [[1, 128]], 1)
    iota("cg1", T.cg1[:], [[1, 8], [0, 16]], 1)
    iota("nv", T.nv[:], [[1, 16]], 1)
    iota("j16", T.j16[:], [[16, 16]], 1, 1)
    iota("ct", T.ct[:], [[0, 16], [CAP, 8]], P - int(BIGS))
    if rank > 0:
        iota("qc", T.qc[:, 0:16 * rank], [[1, rank], [0, 16]], 0, 0, [("qc", 0, 16 * rank)])
    if rank < NO:
        iota("qc", T.qc[:, 16 * rank:112], [[1, NO - rank], [0, 16]], rank + 1, 0, [("qc", 16 * rank, 112)])
    iota("cp", T.cp[:], [[1, 16], [16, 8]], 1)
    iota("d0", T.d0[:], [[0, NO], [1000, 16]])
    iota("dd", T.dd[:], [[0, 16], [4000, 8]])
    iota("cyg", T.cyg[:], [[4, 8], [0, 4], [1, 4]])
    iota("cxg", T.cxg[:], [[4, 8], [1, 4], [0, 4]])
    choose("cxn", "cxg", [[0, 8], [1, 4], [-1, 4]], OP.not_equal, -1.0, 0)
    choose("cy8", "cyg", [[0, 8], [-1, 16]], OP.is_ge, -1.0, 7)
    choose("cgh", "cg1", [[0, 8], [1, 16]], OP.is_ge, -1.0, -8)
    iota("c4", T.c4[:], [[16, 8], [0, 4], [1, 4]], 1)

    sh, an = OP.logical_shift_right, OP.bitwise_and
    K16G, K15, KG1, B2, KFC, M3, B3, PAR, A32, XF = [T.ff[:, c:c + 1] for c in range(10)]
    EARLY_FF, LATE_FF = [("ff", 0, 4)], [("ff", 4, 10)]

    def columns(ints, at, between=lambda: None):
        for c, (src, o0, n0, o1, n1) in enumerate(ints):
            ts(T.fi[:, at + c:at + c + 1], T.ki[:, src:src + 1], n0, None if o1 is None else n1, (o0, o1), full("ki"), [("fi", at + c, at + c + 1)])
        between()
        end = at + len(ints)
        copy(T.ff[:, at:end], T.fi[:, at:end], [("fi", at, end)], [("ff", at, end)])

    def fcol(c):
        return T.fx[:, c:c + 1]

    def dep(*cs):
        return [("fx", c, c + 1) for c in cs]

    def fx(c, in0, s1, s2, *ops):
        ts(fcol(c), in0, s1, s2, ops, EARLY_FF + LATE_FF, dep(c))

    def tile(name, src, col, s2, ops, reads):
        ts(T[name][:], T[src][:], col, s2, ops, full(src) + reads, full(name))

    EQ, EQM = (OP.is_equal,), (OP.is_equal, OP.mult)
    columns([(0, an, 112, None, 0), (0, an, 15, None, 0), (1, sh, 4, None, 0), (0, sh, 2, an, 1)], 0,
            lambda: fill(T.nb[:], 0.0, full("nb")))
    tile("mI", "c1", T.k1[:], None, EQ, full("k1"))
    tile("mU1", "c1", T.k1[:], -1.0, (OP.is_lt, OP.mult), full("k1"))
    tile("mU3", "c1", T.k1[:], BIGS, EQM, full("k1"))
    tile("mU2", "cg1", KG1, None, (OP.is_lt,), EARLY_FF)
    for m in (1, 3, 2):
        mm(T.ppo0[:, 0:128], T.mI[:], T["mU%d" % m][:], m == 1, m == 2, full("mI", "mU%d" % m), full("ppo0"))
    act(T.mU[:], T.ppo0[:, 0:128], ACT.Copy, full("ppo0"), full("mU"))
    tile("mB", "cg1", KG1, None, EQ, EARLY_FF)
    ts(T.bc[:, 0:8], T.nv[:, 0:8], 0.0, K15, (OP.mult, OP.add), full("nv") + EARLY_FF, full("bc"))
    ts(T.k9[:], T.k1[:], 16.0, -7.0, (OP.mult, OP.add), full("k1"), full("k9"))
    for name, b in (("mRH", 0.0), ("mRL", -4.0)):
        ts(T[name][0:8, :], T.c1[0:8, :], b, T.k9[0:8, :], (OP.add, OP.is_equal), full("c1", "k9"), full(name))
    ts(T.ct[:, 7:128:8], T.j16[:], K16G, None, (OP.subtract,), full("j16", "ct") + EARLY_FF, full("ct"))
    fill(T.send[:, P:P + KF], 0.0, [("send", P, P + KF)])

    def owners_to_slots(*between):
        todo = list(between) + [lambda: None] * 4
        tt(T.oo[:], T.ow[:].indirect(T.bc[:, 0:NO]), T.qc[:], OP.is_equal, full("ow", "bc", "qc"), full("oo"))
        mm(T.ppf0[:, 0:112], T.mB[:], T.oo[:], True, True, full("mB", "oo"), full("ppf0"))
        mm(T.ppf1[:, 0:128], T.mI[:], T.ct[:], True, False, full("mI", "ct"), full("ppf1"))
        for d in range(NO):
            mm(T.ppf1[:, d:128:8], T.mU[:], T.oo[:, 16 * d:16 * d + 16], False, False, full("mU", "oo"), full("ppf1"))
        todo[0]()
        do("v", lambda e: e.tensor_tensor_scan(T.sc[:], T.d0[:], T.ppf0[:, 0:112], 0.0, OP.min, OP.add), full("d0", "ppf0"), full("sc"))
        todo[1]()
        for d in range(NO):
            mm(T.ppf1[:, d:128:8], T.mI[:], T.sc[:, 16 * d:16 * d + 16], False, d == NO - 1, full("mI", "sc"), full("ppf1"))
        do("v", lambda e: e.tensor_tensor_scan(T.sx[:], T.dd[:], T.ppf1[:, 0:128], 0.0, OP.min, OP.max), full("dd", "ppf1"), full("sx"))
        todo[2]()
        ts(T.slu[:], T.sx[:, 7:128:8], -1.0, None, (OP.add,), full("sx"), full("slu"))
        todo[3]()

    def remote(land, sem, lsem, src, at, width, to):
        hazards("g", full(src), [])
        tr = []
        for d, q in enumerate(others):
            dst = T.cores[q]
            rid, pid, _ = topo.addr(dst)
            e = topo.engines(core, dst)
            me = rank - (rank > q)
            tr.append(RemoteDMATransfer(dst_ids=[DstId(rid=rid, pnc=pid)], dma_engine_mask=(1 << e[2 * d]) | (1 << e[2 * d + 1]),
                                        remote_sem=T.sem[sem], src=T[src][:, at + width * d:at + width * d + width],
                                        dst=T[land][:, to + width * me:to + width * me + width]))
        g.remote_dma_fused(tr, local_sem=T.sem[lsem])

    def pack_and_send(r):
        if r:
            wait("v", "lq%d" % (r - 1), 2 * NO)
        copy(T.send[:].indirect(T.slu[:]), T.pay[:], full("slu", "pay"), full("send"))
        remote("rq%d" % r, "rqs%d" % r, "lq%d" % r, "send", P, CAP, 0)

    def answer_places():
        ts(T.sl[:], T.sx[:, 7:128:8], -1.0, None, (OP.add,), full("sx"), full("sl"))
        ts(T.si[:], T.sx[:, 7:128:8], 3.0 * P - 1.0, None, (OP.add,), full("sx"), full("si"))
        yield
        ts(T.sj[:], T.si[:], 2, None, (OP.arith_shift_right,), full("si"), full("sj"))
        yield
        tt(T.sm[:], T.sl[:], T.sj[:], OP.min, full("sl", "sj"), full("sm"))
        yield
        copy(T.of2[:], T.sm[:], full("sm"), full("of2"))
        act(T.mask[:], T.tab[:].indirect(T.slu[:]), ACT.Copy, full("tab", "slu"), full("mask"))
        yield

    def cols(name, lo, hi):
        if len(SCRATCH[name][1]) == 2:
            return T[name][:, lo:hi]
        return T[name][:, lo // 16:hi // 16, :]

    def rows_matmul(p, i, z):
        at, _, _, nb = HALVES[p][i]
        pc, n = "pd%s%d" % (p, i), 16 * nb
        for h in range(2):
            for e in range(SUB):
                m = 128 * (2 * e + h)
                if len(SCRATCH[z][1]) == 2:
                    src = T[z][:, at + e * n:at + e * n + n]
                else:
                    src = T[z][:, at // 16 + e:at // 16 + SUB * nb:SUB, :]
                mm(T[pc][:, 0:nb, 16 * h:16 * h + 16], T.mL[:, m:m + 128], src,
                   e == 0, e == SUB - 1, full("mL") + [(z, at, at + SUB * n)], full(pc))

    def rows_transpose(p, i):
        tr, pc, nb = "%str%d" % (p, i), "pd%s%d" % (p, i), HALVES[p][i][3]
        do("v", lambda e: e.transpose(T[tr][:], T[pc][:, 0:nb, :]), full(pc), full(tr))

    def offsets(p, i, blocks=True):
        lc, nb = HALVES[p][i][2:4]
        tr = "%str%d" % (p, i)
        for c, n, src in [(lc, SUB * nb, T[tr][:, :, 0:SUB])] if blocks else [(lc + e * nb, nb, T[tr][:, :, e]) for e in range(SUB)]:
            ts(T[p + "idx"][:, c:c + n], src, float(PADL - OFF - base), float(TT + PADL), (OP.add, OP.min),
               full(tr), [(p + "idx", c, c + n)])

    def walk(p, i, r):
        at, k, lc, _ = HALVES[p][i]
        pd, pp = "pd%s%d" % (p, i), "pp%s%d" % (p, i)
        end = at + k

        def reg(name):
            return [(name, at, end)]
        for s in range(S):
            z = ("pay" if p == "o" else "rq%d" % r) if s == 0 else p + "y"
            y = "win%d" % r if p == "o" and s == S - 1 else p + "y"
            idx = T[p + "idx"][:, lc:lc + k // 16]
            idep = [(p + "idx", lc, lc + k // 16)]
            tt(T[p + "pr"][:, at:end], T.pl[:].indirect(idx), T[p + "crd"][:, at:end], OP.mult, PL + idep + reg(p + "crd"), reg(p + "pr"))
            act(T[p + "nb"][:, at:end], T.nb[:].indirect(idx), ACT.Copy, NB + idep, reg(p + "nb"))
            mm(T[pp][:, 0:k], T.mJ[:], cols(z, at, end), True, False, full("mJ") + reg(z), full(pp))
            yield
            mm(T[pd][:, 0:k // 16, 0:16], T.mA[:], T[p + "pr"][:, at:end], True, True, full("mA") + reg(p + "pr"), full(pd))
            yield
            ts(T[p + "sb"][:, at:end], T[pd][:, 0:k // 16, 0:16], fcol(7), None, (OP.is_ge,), full(pd) + dep(7), reg(p + "sb"))
            yield
            mm(T[pp][:, 0:k], T.mI[:], T[p + "nb"][:, at:end], False, False, full("mI") + reg(p + "nb"), full(pp))
            mm(T[pp][:, 0:k], T.mF[:], T[p + "sb"][:, at:end], False, True, full("mF") + reg(p + "sb"), full(pp))
            yield
            ts(cols(y, at, end), T[pp][:, 0:k], fcol(8), 0.0, (OP.add, OP.max), full(pp) + dep(8), [(y, at, end)])
            yield
            if s < S - 1:
                rows_matmul(p, i, y)
                yield
                rows_transpose(p, i)
                yield
                offsets(p, i)
                yield

    def weave(*parts):
        live = list(parts)
        while live:
            for w in list(live):
                if next(w, 0) == 0:
                    live.remove(w)

    def part(w, n):
        for _ in range(n):
            if next(w, 0) == 0:
                return
            yield

    owns = {}

    def own(r, n, *more):
        if r not in owns:
            owns[r] = [walk("o", i, r) for i in range(2)]
        weave(*[part(w, n) for w in owns[r]], *more)

    def foreign_start(r, i):
        rq = "rq%d" % r
        at, k, _, _ = HALVES["f"][i]
        pp = "ppf%d" % i
        rows_matmul("f", i, rq)
        yield
        mm(T[pp][:, 0:k], T.mC[:], T[rq][:, at:at + k], True, True, full("mC") + [(rq, at, at + k)], full(pp))
        rows_transpose("f", i)
        act(T.fcrd[:, at:at + k], T[pp][:, 0:k], ACT.Identity, full(pp) + dep(9), [("fcrd", at, at + k)], bias=fcol(9))
        yield
        offsets("f", i, False)
        yield
        for _ in walk("f", i, r):
            yield

    def foreign(r):
        wait("t", "rqs%d" % r, 2 * NO)
        live, n = [foreign_start(r, i) for i in range(2)], 0
        while live:
            for w in list(live):
                if next(w, 0) == 0:
                    live.remove(w)
            n += 1
            if n in BETWEEN[r]:
                own(r, 1)
        pk = "pk%d" % r
        for u in range(4):
            mm(T.ppf0[:, 256:300], T.mQ[:, 128 * u:128 * u + 128], T.fy[:, 0:11, u:16:4], u == 0, u == 3, full("mQ", "fy"), full("ppf0"))
        copy(T[pk][:], T.ppf0[:, 256:298], full("ppf0"), full(pk))
        remote("win%d" % r, "rss%d" % r, "lr%d" % r, pk, 0, NR, P)

    def merge(r):
        win = "win%d" % r
        wait("v", "rss%d" % r, 2 * NO)
        for i in range(2):
            at, k, lc, _ = HALVES["o"][i]
            tt(T.gm[:, at:at + k], T[win][:, 0:P + 42].indirect(T.of2[:, lc:lc + 8]), T.mask[:, at:at + k], OP.mult,
               full(win, "of2", "mask"), [("gm", at, at + k)])
            rows_matmul("o", i, "gm")
        for i in range(2):
            rows_transpose("o", i)

    def list_parts():
        for i in range(2):
            for e in range(SUB):
                yield i, T["otr%d" % i][:, :, e], HALVES["o"][i][2] + 4 * e

    copy(T.lhl[:, 0:16], T.l0[:], full("l0"), [("lhl", 0, 16)])
    ts(T.l32[:], T.l0[:], float(OFF), None, (OP.add,), full("l0"), full("l32"))
    ts(T.ow[:], T.l0[:], 10, None, (sh,), full("l0"), full("ow"))
    tt(T.lhl[:, 16:32], T.l32[:], T.lhl[:, 0:16], OP.subtract, full("l32") + [("lhl", 0, 16)], [("lhl", 16, 32)])
    tile("mP", "cp", T.k1[:], None, EQ, full("k1"))
    for i in range(16):
        mm(T.ppo1[0:8, i:512:16], T.mP[:, 8 * i:8 * i + 8], T.lhl[:], True, True, full("mP", "lhl"), full("ppo1"))
    for h in range(2):
        act(T.cx[0:8, P * h:P * h + P], T.ppo1[0:8, P * h:P * h + P], ACT.Copy, full("ppo1"), [("cx", P * h, P * h + P)])

    def high():
        ts(T.xt[:], T.xi[:], B2, None, (OP.mult,), XI + EARLY_FF, full("xt"))

    def lows():
        for lo, hi in ((0, P // 2), (P // 2, P)):
            tt(T.coord[:, lo:hi], T.xi[:, lo:hi], T.xt[:, lo:hi], OP.subtract, XI + full("xt"), [("coord", lo, hi)])

    def codes0():
        copy(T.nbs[:, 0:32], T.nbi[:], full("nbi"), [("nbs", 0, 32)])

    def codes1():
        ts(T.nbf[:], T.nbi[:], float(OFF), None, (OP.add,), full("nbi"), full("nbf"))
        tt(T.nbs[:, 32:64], T.nbf[:], T.nbs[:, 0:32], OP.subtract, full("nbf") + [("nbs", 0, 32)], [("nbs", 32, 64)])
        for h in range(2):
            dma("y", "dnt", T.nbt[128 * h:128 * h + 128, :], T.nbs[:, 32 * h:32 * h + 32], full("nbs"), full("nbt%d" % h), 32)

    owners_to_slots(high, lows, codes0, codes1)
    mm(T.ppo0[:, 0:P], T.mI[:], T.coord[:], True, False, full("mI", "coord"), full("ppo0"))
    mm(T.ppo0[:, 0:P], T.mRH[0:8, :], T.cx[0:8, 0:P], False, False, full("mRH") + [("cx", 0, P)], full("ppo0"))
    mm(T.ppo0[:, 0:P], T.mRL[0:8, :], T.cx[0:8, P:2 * P], False, True, full("mRL") + [("cx", P, 2 * P)], full("ppo0"))
    act(T.pay[:], T.ppo0[:, 0:P], ACT.Identity, full("ppo0"), full("pay"))
    pack_and_send(0)

    iota("s4", T.s4[:], [[0, KF // 4], [1, 4]])
    hazards("y", full("nb"), [])
    for k in range(8):
        dma("y", "dnb", T.nb[16 * k:16 * k + 8, PADL:PADL + TT], T.nbt[:], full("nbt0", "nbt1"), full("nb%d" % k), 128)
    NB = full("nb", *["nb%d" % k for k in range(8)])
    columns([(0, sh, 2, None, 0), (0, an, 3, None, 0), (0, sh, 3, an, 1), (0, sh, 4, an, 1), (0, an, 96, None, 0),
             (0, sh, 2, an, 3)], 4)
    fill(T.pl[:, 0:PADL], 0, [("pl", 0, PADL)])
    fill(T.pl[:, TT + PADL:TW], 0, [("pl", TT + PADL, TW)])
    ts(T.oidx[:], T.l0[:], float(PADL - base), float(TT + PADL), (OP.add, OP.min), full("l0"), full("oidx"))
    fx(13, B2, 4.0, K16G, OP.mult, OP.add)
    fx(14, B3, -1.0, 1.0, OP.mult, OP.add)
    ts(fcol(10), M3, 0.0, fcol(14), (OP.is_equal, OP.max), LATE_FF + dep(14), dep(10))
    tt(fcol(7), XF, M3, OP.is_gt, LATE_FF, dep(7))
    tt(fcol(15), XF, M3, OP.is_equal, LATE_FF, dep(15))
    fx(8, B3, -BIG, -3.0 * BIG, OP.mult, OP.add)
    fx(9, M3, 3.0, None, OP.is_equal)
    ts(fcol(16), K16G, M3, B3, (OP.add, OP.mult), EARLY_FF + LATE_FF, dep(16))
    fx(18, PAR, -1.0, 1.0, OP.mult, OP.add)
    ts(fcol(17), fcol(15), -2.0 * BIG, BIG, (OP.mult, OP.add), dep(15), dep(17))
    tt(fcol(19), KG1, fcol(15), OP.mult, EARLY_FF + dep(15), dep(19))
    tt(fcol(11), fcol(10), fcol(18), OP.mult, dep(10, 18), dep(11))
    tt(fcol(12), fcol(10), PAR, OP.mult, LATE_FF + dep(10), dep(12))
    tile("mC", "c4", fcol(16), None, EQ, dep(16))
    ts(T.tau[:, 0:9], T.nv[:, 0:9], fcol(13), fcol(10), (OP.add, OP.mult), full("nv") + dep(10, 13), full("tau"))
    tile("mA1", "cyg", KFC, None, EQ, LATE_FF)
    tile("mA2", "cxn", KFC, None, EQ, LATE_FF)
    tile("mF1", "cy8", KFC, fcol(17), EQM, LATE_FF + dep(17))
    tile("mF2", "cgh", fcol(19), BIG, EQM, dep(19))
    for h in range(2):
        ts(T.tal[:, 2 * h:2 * h + 2], T.nv[:, 0:2], A32, fcol(11 + h), (OP.add, OP.mult), full("nv") + LATE_FF + dep(11 + h), [("tal", 2 * h, 2 * h + 2)])
    tt(T.mA[:], T.mA1[:], T.mA2[:], OP.subtract, full("mA1", "mA2"), full("mA"))
    tt(T.mF[:], T.mF1[:], T.mF2[:], OP.add, full("mF1", "mF2"), full("mF"))
    tile("mJ", "c1", T.tau[:, 8:9], None, EQ, full("tau"))
    mm(T.ppo0[:, 0:P], T.mC[:], T.coord[:], True, True, full("mC", "coord"), full("ppo0"))
    act(T.ocrd[:], T.ppo0[:, 0:P], ACT.Identity, full("ppo0") + dep(9), full("ocrd"), bias=fcol(9))
    for e in range(2):
        for h in range(2):
            at = 128 * (2 * e + h)
            ts(T.mL[:, at:at + 128], T.c1[:], T.tal[:, 2 * h + e:2 * h + e + 1], None, EQ, full("c1", "tal"), [("mL", at, at + 128)])
    for r in range(R):
        fill(T["rq%d" % r][:, KF:KW], 0.0, full("rq%d" % r))
    fill(cols("fy", 176, KW), 0.0, [("fy", 176, KW)])
    act(T.tab[:, 0:P], T.pay[:], ACT.Identity, full("pay") + dep(10), [("tab", 0, P)], scale=0.0, bias=fcol(10))
    act(T.ds[:], T.s4[:], ACT.Abs, full("s4") + LATE_FF, full("ds"), scale=-1.0, bias=M3)
    for u in range(4):
        act(T["dq%d" % u][:], T.c1[:], ACT.Abs, full("c1", "tau"), full("dq%d" % u), scale=-1.0, bias=T.tau[:, u:u + 1])
    act(T.tab[:, P:P + KF], T.ds[:], ACT.Relu, full("ds") + dep(14), [("tab", P, P + KF)], scale=-1.0, bias=fcol(14))

    def answer_matrices():
        for u in range(4):
            act(T.mQ[:, 128 * u:128 * u + 128], T["dq%d" % u][:], ACT.Relu, full("dq%d" % u), [("mQ", 128 * u, 128 * u + 128)], scale=-1.0, bias=1.0)
            yield

    for r in range(R):
        own(r, STAGES[r], answer_places(), *([answer_matrices()] if r == 0 else []))
        foreign(r)
        own(r, 8 * S)
        merge(r)
        if r + 1 < R:
            for i, src, c in list_parts():
                ts(T.ow[:, c:c + 4], src, 1.0 / TT, -(OFF + 511.5) / TT, (OP.mult, OP.add), full("otr%d" % i), [("ow", c, c + 4)])
            mm(T.ppo0[:, 0:P], T.mI[:], T.coord[:], True, False, full("mI", "coord"), full("ppo0"))
            mm(T.ppo0[:, 0:P], T.mI[:], T.gm[:], False, True, full("mI", "gm"), full("ppo0"))
            act(T.pay[:], T.ppo0[:, 0:P], ACT.Identity, full("ppo0"), full("pay"))
            owners_to_slots()
            pack_and_send(r + 1)
            offsets("o", 0, False)
            offsets("o", 1, False)
        else:
            for i, src, c in list_parts():
                ts(T.yl[:, c:c + 4], src, -float(OFF), None, (OP.add,), full("otr%d" % i), [("yl", c, c + 4)])
            dma("y", "dy", T.y[:], T.yl[:], full("yl"), [], 16)
    for sem in ("ct", "cs", "cg"):
        wait("g", sem, count[sem])
    for sem in ("cv", "dl0", "dni", "dxi", "dpl", "dnt", "dnb", "dy"):
        wait("y", sem, count[sem])
    for r in range(R):
        wait("g", "lq%d" % r, 2 * NO)
        wait("g", "lr%d" % r, 2 * NO)
